import numpy as np, ml_dtypes
CORES = [4,20,36,52,68,84,100,116,132,148,164,180,196,212,228,244]
N = 16
TOK, K = 512, 2
ROUTE = [[[1,6],[2,6],[8,10],[8,12],[8,10],[3,4],[2,6],[0,10],[1,15],[8,10],[1,3],[6,11],[0,14],[13,14],[2,14],[1,13],[8,9],[3,6],[6,14],[10,11],[6,7],[2,7],[5,14],[7,13],[2,6],[3,10],[2,6],[2,9],[8,14],[4,6],[1,2],[2,12],[6,12],[1,7],[9,13],[2,11],[6,9],[12,15],[0,2],[10,11],[4,7],[3,14],[6,15],[4,7],[0,2],[1,3],[5,7],[1,12],[8,12],[2,9],[1,2],[6,12],[5,7],[1,14],[5,11],[2,4],[11,15],[2,15],[9,15],[4,14],[0,13],[3,6],[5,15],[8,12],[5,7],[10,12],[7,8],[6,15],[4,6],[10,11],[7,14],[0,14],[6,14],[2,5],[9,12],[2,11],[9,14],[4,5],[3,9],[0,15],[10,15],[2,9],[3,13],[1,2],[3,10],[1,12],[3,14],[6,11],[9,13],[0,8],[0,13],[4,7],[4,12],[10,13],[6,7],[3,14],[1,15],[11,13],[7,12],[2,6],[3,9],[4,6],[1,11],[6,13],[7,9],[4,6],[1,15],[0,12],[7,13],[1,7],[4,7],[12,14],[2,4],[1,15],[2,5],[1,12],[5,12],[2,11],[7,13],[8,14],[3,8],[2,13],[2,3],[4,10],[2,12],[6,10],[0,11],[1,5],[6,7],[1,14],[2,13],[14,15],[5,7],[13,15],[5,7],[4,9],[0,6],[0,2],[3,6],[11,13],[7,9],[7,11],[8,12],[8,14],[3,5],[3,8],[2,8],[3,12],[1,9],[3,8],[12,13],[9,10],[9,15],[11,12],[3,5],[8,13],[4,9],[0,15],[6,9],[1,3],[9,14],[5,10],[7,14],[1,13],[1,5],[6,7],[7,9],[5,13],[7,15],[6,12],[6,12],[1,9],[1,14],[12,13],[3,14],[11,12],[3,12],[0,1],[1,5],[7,13],[7,11],[12,15],[2,10],[2,12],[3,11],[1,6],[8,14],[2,8],[2,6],[3,6],[2,8],[2,6],[7,8],[0,4],[9,14],[2,13],[0,13],[2,14],[5,6],[9,12],[0,5],[0,1],[0,13],[1,14],[3,15],[3,9],[0,14],[6,15],[8,11],[0,15],[3,13],[2,13],[4,5],[6,7],[3,7],[2,12],[6,11],[0,15],[4,7],[0,10],[11,14],[1,15],[2,6],[0,2],[0,8],[10,14],[0,5],[3,15],[0,2],[6,12],[0,7],[3,11],[10,12],[8,14],[7,12],[0,4],[4,7],[7,13],[6,13],[0,13],[4,12],[3,7],[0,7],[3,4],[1,5],[12,14],[3,6],[4,14],[6,7],[9,10],[2,6],[0,3],[9,10],[3,13],[0,7],[8,13],[4,13],[9,13],[5,11],[1,5],[1,15],[10,13],[3,5],[2,14],[9,15],[0,11],[1,12],[2,3],[3,7],[6,13],[0,10],[5,7],[3,9],[1,13],[0,1],[3,14],[4,7],[4,8],[11,14],[10,14],[4,11],[5,9],[6,12],[10,13],[10,15],[2,12],[8,14],[1,9],[1,13],[10,12],[4,11],[10,15],[0,7],[0,13],[1,12],[11,13],[12,15],[11,12],[5,11],[8,13],[2,14],[11,15],[0,1],[3,15],[3,5],[2,5],[1,9],[0,3],[9,12],[13,15],[4,6],[0,12],[2,4],[4,6],[1,5],[3,13],[3,11],[2,10],[4,13],[12,13],[3,7],[7,13],[4,14],[5,7],[2,9],[5,11],[11,12],[12,14],[8,13],[6,8],[9,13],[5,11],[5,7],[0,6],[11,15],[4,8],[4,15],[0,2],[6,9],[3,5],[1,8],[2,12],[0,5],[1,14],[3,10],[4,13],[6,15],[2,15],[3,8],[12,14],[12,15],[7,13],[3,6],[0,11],[3,13],[0,15],[0,3],[5,12],[1,11],[10,11],[3,6],[7,9],[4,5],[2,6],[8,14],[2,10],[6,7],[6,7],[3,11],[13,15],[8,13],[9,12],[10,14],[0,9],[2,10],[0,7],[3,14],[8,11],[8,10],[7,14],[1,11],[2,15],[1,9],[3,7],[1,13],[2,5],[0,1],[0,4],[4,10],[0,12],[2,12],[1,10],[7,13],[0,13],[0,10],[3,8],[0,6],[1,12],[12,15],[5,6],[2,13],[3,14],[5,11],[3,7],[3,10],[2,7],[12,13],[5,15],[9,14],[4,5],[5,8],[3,6],[3,5],[1,5],[8,14],[7,14],[6,11],[0,8],[4,10],[13,15],[7,13],[0,14],[8,11],[2,11],[1,7],[10,12],[2,14],[0,6],[6,12],[2,10],[6,7],[10,15],[4,8],[3,9],[2,7],[3,8],[8,13],[11,14],[3,11],[1,6],[10,13],[4,11],[5,7],[11,14],[7,9],[3,11],[5,15],[1,11],[7,12],[0,9],[6,12],[0,13],[8,10],[4,15],[5,15],[2,9],[4,11],[1,8],[1,6],[1,10],[1,12],[5,11],[0,12],[9,15],[4,8],[3,5],[3,12],[2,7],[3,15],[8,13],[3,8],[11,12],[3,8],[0,10],[2,14],[0,7],[2,10],[8,11],[3,13],[8,13],[1,13],[4,8],[5,6],[10,15],[5,14],[3,12],[1,10],[2,6],[3,12],[3,6],[6,15],[3,8],[8,14],[1,4],[3,10],[1,10],[14,15],[8,14],[14,15],[4,8],[0,7],[0,4],[0,1],[5,11],[8,13],[0,5],[5,12],[3,14],[12,14],[8,10],[9,11],[4,11]],[[5,10],[13,14],[2,14],[4,6],[13,15],[1,10],[4,8],[8,12],[5,12],[6,9],[0,3],[2,14],[8,10],[9,12],[11,14],[10,14],[1,13],[4,12],[1,13],[6,15],[0,4],[8,12],[1,8],[2,3],[3,7],[1,10],[4,10],[5,12],[12,15],[1,4],[4,5],[1,6],[3,15],[6,8],[2,9],[4,15],[2,8],[2,6],[7,12],[5,14],[10,13],[0,15],[1,14],[3,13],[8,10],[3,14],[3,5],[1,10],[8,9],[1,4],[3,14],[14,15],[2,15],[2,3],[4,15],[7,10],[9,12],[3,9],[4,6],[13,14],[8,11],[10,13],[0,5],[3,5],[3,8],[0,10],[5,7],[5,7],[5,12],[4,13],[5,13],[2,12],[9,10],[4,6],[6,8],[3,9],[2,8],[4,6],[7,12],[11,12],[6,13],[2,12],[10,11],[11,13],[0,2],[4,15],[12,14],[0,7],[9,14],[0,11],[4,6],[2,3],[0,1],[2,8],[0,9],[0,12],[2,14],[2,11],[4,7],[5,11],[11,14],[5,6],[5,6],[9,13],[1,15],[5,14],[10,11],[6,10],[2,11],[13,14],[2,10],[11,12],[5,14],[4,13],[10,13],[3,6],[4,14],[5,11],[4,10],[12,15],[1,14],[0,13],[0,7],[0,13],[3,11],[12,14],[2,14],[0,3],[4,8],[9,11],[5,12],[8,9],[4,11],[4,12],[2,4],[0,8],[12,13],[8,9],[1,9],[10,11],[1,8],[4,6],[3,7],[0,15],[1,7],[2,7],[1,15],[12,15],[1,9],[5,6],[4,12],[4,8],[5,11],[5,6],[2,13],[6,10],[0,15],[4,11],[7,15],[13,14],[8,10],[1,7],[1,13],[4,5],[1,7],[1,11],[3,7],[0,10],[0,7],[10,14],[5,12],[12,14],[5,11],[4,10],[5,11],[9,10],[7,8],[2,8],[0,10],[2,7],[2,6],[5,13],[3,8],[3,5],[12,14],[2,3],[5,6],[0,10],[10,11],[3,14],[2,15],[12,14],[7,8],[2,10],[0,13],[0,9],[6,8],[5,11],[5,15],[2,13],[12,13],[5,10],[2,3],[1,14],[5,12],[6,11],[7,10],[3,13],[1,6],[13,14],[1,11],[1,6],[11,12],[9,12],[6,8],[0,12],[3,12],[10,15],[1,4],[0,15],[4,5],[9,14],[2,4],[1,11],[3,10],[3,6],[3,11],[11,13],[4,7],[5,10],[0,11],[2,10],[1,5],[2,15],[1,5],[0,3],[2,9],[0,9],[1,3],[5,7],[2,12],[0,13],[3,13],[2,12],[5,6],[2,10],[4,13],[5,7],[5,10],[4,12],[8,14],[7,15],[3,15],[7,8],[6,11],[5,7],[2,4],[5,8],[3,12],[1,7],[4,11],[2,11],[0,13],[2,7],[9,12],[7,10],[6,12],[2,4],[4,15],[7,15],[1,9],[1,15],[8,13],[13,15],[10,14],[6,15],[4,12],[6,13],[2,10],[5,14],[5,8],[0,5],[0,4],[12,13],[7,11],[1,10],[4,7],[7,11],[6,9],[5,11],[1,15],[8,15],[5,9],[4,12],[1,3],[5,13],[5,13],[3,9],[0,7],[1,7],[1,8],[1,13],[11,14],[1,10],[3,9],[11,13],[5,13],[2,15],[1,5],[1,7],[3,13],[9,15],[4,10],[3,5],[0,15],[6,11],[5,9],[11,15],[7,15],[11,12],[0,3],[4,8],[13,14],[0,15],[0,15],[0,8],[10,13],[2,9],[2,3],[0,9],[8,12],[3,6],[2,7],[1,11],[4,8],[10,15],[9,13],[3,15],[0,1],[14,15],[4,15],[4,15],[13,14],[2,10],[10,13],[7,8],[9,12],[10,12],[1,10],[6,7],[5,7],[9,12],[6,10],[4,12],[3,7],[8,14],[4,9],[4,8],[6,9],[9,11],[7,9],[0,15],[1,9],[11,14],[0,2],[2,3],[8,12],[5,8],[5,12],[1,4],[2,9],[13,14],[10,14],[12,15],[3,5],[3,13],[11,14],[13,14],[7,11],[4,15],[1,4],[3,10],[0,14],[0,13],[4,8],[10,13],[12,13],[8,14],[6,12],[8,15],[3,11],[6,12],[1,2],[8,15],[3,6],[1,10],[9,14],[9,14],[0,15],[13,14],[4,13],[9,10],[1,6],[10,11],[2,10],[6,13],[10,11],[0,5],[0,14],[1,9],[5,12],[6,12],[9,10],[5,13],[4,8],[5,10],[2,3],[0,11],[4,9],[9,15],[1,15],[4,14],[0,13],[7,8],[5,12],[0,13],[2,3],[10,11],[11,15],[3,10],[1,9],[2,10],[1,14],[4,14],[1,3],[0,4],[4,11],[2,15],[0,13],[13,15],[9,13],[11,12],[14,15],[6,8],[8,13],[2,15],[0,7],[11,13],[10,15],[6,10],[5,11],[6,15],[3,13],[12,13],[7,14],[1,15],[13,15],[7,15],[5,10],[7,15],[0,7],[4,6],[8,11],[0,14],[2,8],[1,15],[1,11],[1,14],[4,9],[1,4],[1,5],[3,15],[4,9],[2,12],[3,9],[4,5],[12,13],[3,13],[5,13],[6,9],[2,6],[7,9],[6,14],[11,15],[4,9],[4,6],[3,8],[7,12],[3,15],[11,12],[9,10],[2,4],[2,4],[12,13],[1,2],[6,10],[7,8],[2,11],[7,13],[13,15],[4,5],[4,8],[1,12],[11,12],[13,15],[1,3],[11,13],[0,14],[3,14],[1,11],[13,14],[6,14]],[[1,14],[0,8],[2,13],[0,15],[8,10],[5,13],[5,6],[4,6],[5,8],[0,8],[4,7],[6,13],[5,9],[5,10],[0,13],[0,5],[4,10],[2,13],[1,15],[0,11],[0,12],[8,11],[2,10],[0,9],[8,12],[3,15],[9,15],[9,10],[10,14],[2,8],[12,13],[12,14],[3,13],[12,15],[2,8],[6,13],[10,13],[5,13],[12,15],[0,11],[4,5],[5,14],[4,9],[11,12],[6,12],[7,14],[5,9],[0,6],[14,15],[11,13],[9,12],[9,12],[3,13],[8,13],[11,14],[0,13],[6,15],[10,15],[2,14],[12,14],[1,6],[8,11],[1,6],[11,13],[5,14],[4,12],[4,11],[5,8],[0,12],[14,15],[11,12],[0,4],[1,13],[0,7],[4,8],[4,13],[3,14],[3,4],[11,12],[3,6],[8,10],[4,6],[1,13],[0,4],[10,12],[5,8],[1,12],[4,14],[6,15],[7,11],[4,6],[8,14],[8,10],[4,7],[5,7],[9,13],[0,5],[4,10],[1,9],[9,13],[1,5],[4,7],[4,7],[0,3],[6,7],[3,13],[6,15],[7,14],[4,11],[4,14],[3,4],[13,15],[7,11],[5,13],[1,14],[3,14],[7,8],[5,14],[1,12],[12,15],[3,10],[10,13],[4,9],[8,12],[2,13],[4,10],[8,9],[2,9],[12,14],[6,11],[0,2],[6,7],[0,11],[8,12],[2,12],[2,10],[2,4],[3,12],[8,15],[13,14],[1,4],[8,15],[4,12],[2,11],[7,12],[2,5],[4,15],[7,10],[8,11],[9,14],[5,12],[4,9],[10,14],[5,7],[1,3],[11,13],[8,9],[6,7],[14,15],[3,4],[2,10],[1,8],[11,12],[5,10],[12,15],[3,7],[9,11],[1,14],[9,10],[9,14],[8,10],[2,3],[11,14],[5,11],[5,6],[2,4],[1,13],[12,14],[0,10],[7,10],[11,12],[4,11],[4,10],[1,3],[1,10],[2,3],[3,5],[3,8],[1,12],[1,6],[9,15],[9,11],[2,12],[1,12],[8,13],[10,14],[10,13],[8,13],[0,11],[7,15],[5,13],[7,15],[6,15],[7,10],[10,13],[10,15],[1,7],[4,9],[4,11],[2,8],[0,1],[10,14],[2,3],[1,4],[5,12],[13,15],[1,14],[0,7],[1,5],[6,10],[9,13],[1,13],[6,14],[14,15],[5,6],[8,15],[3,6],[1,11],[3,10],[3,5],[12,13],[5,13],[2,6],[5,14],[11,14],[2,15],[0,9],[5,7],[7,8],[5,6],[0,11],[6,7],[10,15],[2,6],[3,7],[8,9],[5,6],[14,15],[8,9],[7,13],[2,5],[7,13],[9,12],[3,7],[13,14],[3,14],[3,5],[1,11],[10,14],[5,14],[6,9],[1,13],[13,14],[10,11],[11,12],[1,15],[3,8],[0,2],[0,9],[4,8],[3,8],[4,14],[6,13],[4,12],[3,4],[5,13],[7,13],[8,15],[5,11],[8,10],[2,13],[5,9],[1,7],[2,13],[1,5],[7,9],[7,9],[4,8],[9,13],[8,9],[2,5],[5,14],[7,9],[0,11],[8,14],[1,9],[0,11],[8,12],[2,3],[2,5],[6,13],[7,15],[3,14],[0,13],[4,10],[2,7],[14,15],[0,9],[5,7],[4,8],[4,13],[7,11],[4,8],[2,5],[14,15],[10,13],[8,13],[7,13],[6,13],[0,15],[0,15],[2,15],[8,12],[0,6],[3,8],[7,8],[3,8],[5,10],[1,7],[8,12],[3,5],[10,11],[9,10],[8,15],[0,8],[4,15],[5,7],[6,14],[0,4],[5,12],[7,11],[5,12],[6,10],[3,12],[11,15],[7,15],[11,12],[4,10],[2,3],[0,15],[10,11],[5,11],[0,10],[7,11],[12,13],[10,15],[2,11],[0,11],[3,11],[10,12],[7,8],[1,10],[14,15],[6,13],[3,10],[4,11],[5,13],[0,13],[7,13],[0,7],[12,15],[1,7],[8,13],[7,15],[6,10],[3,5],[3,5],[0,8],[9,11],[3,14],[7,8],[6,10],[3,12],[3,9],[8,12],[11,12],[8,12],[0,2],[2,15],[2,12],[4,6],[0,14],[0,9],[2,5],[7,8],[0,10],[9,12],[1,9],[1,11],[0,9],[3,10],[0,1],[1,11],[2,15],[2,11],[0,6],[3,10],[3,12],[4,14],[4,8],[5,15],[2,7],[4,7],[1,15],[4,6],[6,13],[6,12],[1,13],[9,15],[2,12],[3,11],[7,9],[2,10],[2,13],[2,12],[8,9],[14,15],[13,14],[9,13],[12,13],[1,4],[1,7],[3,6],[5,15],[8,15],[2,11],[6,15],[5,15],[6,9],[5,14],[1,3],[3,8],[6,14],[6,11],[1,6],[3,10],[3,11],[2,13],[11,12],[1,2],[5,13],[3,7],[10,14],[8,12],[1,14],[9,10],[4,14],[5,7],[0,14],[0,12],[2,8],[1,8],[11,14],[0,1],[0,3],[1,14],[3,10],[0,14],[10,13],[0,10],[13,14],[1,3],[1,9],[14,15],[9,14],[4,14],[1,6],[0,11],[3,13],[3,13],[3,6],[0,13],[2,10],[4,15],[4,6],[0,13],[2,6],[12,14],[5,13],[6,13],[9,14],[0,4],[4,7],[1,7],[8,10],[13,15],[9,13],[1,7],[7,9],[7,9],[1,12],[5,6],[4,11],[13,14],[3,7],[5,7],[9,12],[5,13],[2,9],[5,6],[2,14],[9,11]],[[2,3],[1,11],[3,5],[7,13],[0,8],[1,5],[0,6],[1,7],[14,15],[10,15],[11,12],[6,13],[2,6],[5,6],[10,13],[2,10],[5,9],[5,12],[8,13],[8,14],[1,6],[4,12],[12,15],[3,6],[7,11],[0,15],[2,4],[3,13],[3,13],[0,15],[1,11],[6,14],[6,12],[2,4],[2,9],[4,6],[9,14],[3,5],[1,13],[2,3],[1,7],[9,13],[2,15],[0,5],[3,13],[2,9],[9,13],[0,8],[7,11],[6,12],[7,14],[4,15],[5,15],[2,14],[3,6],[2,13],[0,8],[7,13],[12,14],[10,11],[0,10],[2,10],[4,15],[8,10],[7,12],[11,15],[10,12],[7,11],[10,14],[2,10],[1,2],[14,15],[12,14],[1,14],[9,15],[13,14],[13,14],[4,13],[0,1],[4,15],[2,6],[2,3],[2,5],[4,14],[6,8],[4,6],[1,8],[5,10],[3,11],[2,15],[9,11],[8,14],[1,11],[1,15],[6,13],[3,12],[7,10],[10,15],[3,4],[2,3],[7,15],[3,15],[4,14],[0,9],[4,12],[3,5],[11,13],[7,14],[6,10],[13,14],[2,15],[1,12],[1,2],[3,14],[3,9],[1,15],[0,4],[3,8],[1,10],[0,7],[1,11],[5,11],[9,14],[6,9],[14,15],[6,12],[0,14],[11,12],[3,15],[4,8],[1,13],[6,14],[13,14],[5,15],[4,15],[2,13],[3,14],[1,6],[9,10],[7,9],[1,5],[5,6],[7,8],[4,8],[2,11],[7,9],[10,15],[4,8],[2,5],[4,12],[11,14],[0,7],[0,3],[1,3],[1,4],[5,12],[10,15],[5,11],[5,9],[11,12],[11,12],[9,12],[2,3],[2,13],[8,13],[7,9],[3,12],[9,14],[4,15],[0,6],[4,10],[8,11],[2,5],[11,12],[4,14],[1,11],[9,14],[8,15],[8,9],[6,9],[5,15],[13,14],[10,13],[5,12],[0,9],[8,14],[6,12],[4,11],[0,3],[2,4],[0,8],[9,15],[9,13],[1,11],[7,11],[3,8],[10,15],[8,9],[5,11],[3,15],[1,2],[10,14],[0,8],[1,2],[4,15],[2,13],[5,13],[9,11],[6,8],[4,9],[13,15],[12,15],[5,12],[4,13],[6,14],[3,10],[2,9],[1,7],[7,10],[7,14],[4,10],[8,13],[5,15],[5,14],[9,14],[4,5],[0,8],[9,10],[4,12],[13,14],[7,10],[4,5],[2,12],[7,13],[6,14],[10,11],[8,14],[4,8],[4,8],[11,15],[10,13],[2,13],[10,13],[12,14],[7,11],[4,11],[14,15],[6,11],[2,7],[10,13],[1,5],[1,13],[7,13],[7,13],[3,12],[1,15],[3,14],[2,5],[0,7],[5,6],[7,14],[4,7],[9,13],[2,6],[8,11],[1,2],[4,8],[0,4],[13,14],[9,15],[10,15],[9,13],[0,6],[0,1],[2,6],[3,7],[1,6],[0,12],[10,14],[2,15],[4,13],[1,3],[2,5],[3,6],[0,15],[1,14],[7,13],[5,14],[11,14],[3,13],[7,13],[2,15],[8,12],[11,14],[2,3],[4,5],[2,13],[6,8],[8,10],[0,11],[2,11],[11,14],[6,12],[2,8],[13,15],[2,14],[5,13],[2,10],[11,12],[3,15],[1,4],[4,13],[3,4],[4,11],[1,4],[6,8],[0,6],[2,15],[1,3],[0,6],[1,5],[2,3],[0,5],[0,2],[0,13],[0,6],[2,15],[0,7],[6,9],[11,14],[8,11],[6,9],[2,13],[12,13],[5,11],[0,2],[2,5],[9,14],[6,10],[0,10],[11,13],[8,9],[1,11],[9,13],[13,14],[8,14],[7,10],[13,14],[0,3],[3,8],[0,3],[2,9],[2,10],[0,12],[4,5],[8,10],[0,4],[1,7],[5,7],[1,12],[5,12],[4,12],[5,14],[2,11],[5,7],[6,10],[1,14],[9,14],[3,13],[4,15],[0,9],[0,12],[9,14],[9,15],[8,10],[7,12],[1,4],[9,14],[10,11],[0,15],[2,14],[7,9],[3,4],[0,10],[1,3],[0,13],[2,9],[11,12],[5,11],[1,12],[0,1],[6,13],[6,9],[0,2],[0,8],[9,13],[4,12],[2,12],[5,9],[1,6],[4,10],[7,9],[5,8],[0,8],[7,14],[1,2],[6,15],[2,15],[4,7],[5,12],[10,11],[9,11],[7,13],[8,13],[1,13],[1,10],[5,8],[7,14],[0,5],[10,11],[1,15],[9,13],[2,11],[12,15],[3,6],[4,9],[1,15],[1,4],[0,10],[8,11],[3,15],[7,15],[1,11],[8,14],[7,15],[3,10],[4,9],[0,6],[6,11],[11,13],[7,13],[4,11],[4,10],[5,10],[1,9],[11,15],[7,14],[4,11],[5,12],[6,13],[7,10],[2,5],[1,4],[2,7],[8,10],[2,13],[0,5],[9,13],[4,5],[1,2],[9,11],[8,9],[7,8],[0,1],[4,10],[13,15],[5,13],[7,15],[4,13],[0,1],[7,15],[11,14],[2,10],[4,6],[5,9],[4,7],[2,13],[4,6],[13,14],[1,14],[5,6],[6,9],[7,14],[1,8],[3,13],[3,15],[9,14],[0,13],[3,7],[4,12],[10,13],[3,12],[13,14],[3,5],[3,11],[3,11],[10,11],[5,12],[5,9],[0,7],[10,13],[11,13],[2,11],[2,11],[0,7],[9,13],[12,15],[8,9],[4,15],[6,12],[1,15],[13,15]],[[0,2],[1,12],[7,14],[11,12],[2,8],[3,11],[11,14],[4,15],[5,10],[14,15],[9,13],[2,3],[3,6],[2,14],[11,15],[1,2],[5,7],[11,12],[1,6],[1,2],[5,7],[0,13],[0,11],[6,12],[9,12],[3,10],[10,12],[3,4],[0,10],[1,4],[5,8],[5,12],[10,13],[0,11],[5,9],[14,15],[5,11],[1,10],[5,12],[1,13],[3,10],[0,2],[6,15],[3,9],[5,7],[0,8],[2,3],[6,10],[4,6],[10,15],[2,10],[8,10],[6,15],[2,11],[7,10],[0,13],[1,12],[6,7],[4,15],[8,11],[1,5],[4,9],[1,10],[0,4],[1,11],[9,13],[0,5],[1,3],[10,11],[1,9],[2,8],[6,10],[2,3],[0,10],[7,11],[4,9],[9,12],[7,8],[8,12],[1,5],[2,3],[10,12],[3,8],[1,6],[10,14],[3,15],[0,15],[4,5],[6,11],[0,11],[8,15],[4,11],[3,9],[7,15],[9,12],[4,8],[0,11],[3,9],[4,14],[3,9],[4,10],[9,15],[8,13],[6,11],[7,11],[6,7],[9,15],[4,11],[2,13],[9,14],[4,5],[3,11],[0,5],[5,7],[10,13],[10,12],[0,15],[2,15],[4,14],[4,11],[0,6],[11,14],[0,14],[5,9],[13,14],[1,11],[9,14],[10,13],[8,9],[7,8],[1,5],[0,15],[1,9],[5,15],[10,13],[10,12],[9,11],[11,14],[3,11],[3,14],[9,13],[3,12],[4,11],[12,13],[7,11],[7,11],[2,13],[0,8],[4,5],[5,7],[7,12],[0,1],[8,11],[1,9],[0,5],[11,13],[0,10],[2,11],[0,1],[6,7],[8,9],[6,12],[8,12],[3,11],[3,4],[5,14],[0,11],[8,13],[1,11],[9,15],[9,14],[1,5],[8,9],[9,14],[1,8],[1,9],[11,13],[2,13],[5,15],[8,10],[2,10],[7,11],[0,5],[9,15],[0,6],[9,10],[4,11],[5,6],[9,11],[7,9],[8,13],[11,13],[10,14],[0,15],[10,15],[1,6],[6,15],[0,3],[1,15],[2,7],[5,10],[1,9],[2,9],[4,15],[3,6],[8,10],[4,8],[2,5],[11,14],[9,11],[8,14],[1,10],[9,10],[8,12],[9,14],[8,14],[2,3],[7,15],[2,12],[8,11],[0,4],[9,14],[10,11],[1,4],[4,10],[4,15],[10,13],[8,12],[0,8],[8,11],[6,9],[8,13],[6,15],[4,13],[6,15],[4,8],[0,15],[4,15],[4,6],[12,13],[8,13],[13,15],[5,12],[6,9],[3,15],[1,9],[6,12],[5,7],[12,13],[7,15],[3,5],[9,15],[5,14],[0,1],[3,8],[10,11],[1,8],[4,11],[2,15],[2,9],[10,12],[4,9],[5,11],[5,10],[4,8],[4,12],[6,14],[1,3],[1,9],[5,15],[12,13],[4,6],[1,9],[4,8],[3,5],[4,5],[2,12],[14,15],[0,6],[11,12],[7,14],[5,15],[6,15],[7,8],[0,5],[11,13],[2,12],[10,13],[1,9],[7,14],[2,8],[10,12],[0,6],[2,10],[1,9],[0,7],[10,15],[11,12],[4,13],[2,10],[0,4],[2,12],[8,10],[0,10],[14,15],[4,14],[5,6],[11,15],[7,13],[9,13],[12,13],[5,7],[7,11],[3,10],[10,13],[12,15],[1,15],[1,9],[0,6],[8,12],[10,12],[13,14],[6,10],[1,10],[5,13],[2,5],[5,11],[10,13],[8,10],[0,3],[0,10],[1,7],[5,14],[10,13],[7,13],[3,6],[1,5],[6,14],[5,15],[5,15],[0,5],[6,12],[12,15],[7,15],[5,10],[3,5],[10,13],[0,15],[10,13],[2,14],[5,10],[9,15],[7,8],[2,4],[0,1],[4,10],[10,14],[2,14],[4,12],[5,15],[0,3],[2,13],[5,6],[3,7],[4,11],[1,4],[6,7],[7,14],[0,15],[0,13],[12,14],[3,10],[1,6],[11,13],[3,10],[1,5],[4,15],[1,10],[2,7],[5,6],[2,5],[4,12],[10,15],[2,6],[4,7],[0,15],[2,6],[5,11],[10,13],[10,12],[0,8],[8,11],[10,14],[2,6],[6,7],[10,13],[10,13],[9,12],[2,12],[2,9],[7,9],[2,12],[0,7],[0,10],[2,14],[2,13],[0,6],[7,15],[8,15],[1,8],[8,10],[11,14],[0,8],[0,9],[4,14],[1,12],[7,9],[8,13],[0,2],[0,7],[2,4],[12,14],[3,11],[2,11],[4,9],[0,2],[6,8],[6,12],[2,4],[13,15],[2,13],[5,7],[8,11],[2,15],[1,9],[3,13],[2,12],[1,14],[5,10],[13,14],[1,15],[5,15],[1,15],[2,5],[1,9],[6,13],[2,15],[3,13],[0,8],[11,14],[12,15],[4,15],[4,9],[2,5],[2,7],[8,10],[5,8],[9,11],[6,7],[0,4],[1,6],[9,14],[1,9],[9,14],[4,10],[2,6],[4,13],[10,14],[12,14],[6,9],[4,11],[8,12],[10,15],[11,14],[4,5],[2,8],[1,6],[0,2],[0,2],[1,5],[1,8],[5,8],[10,14],[9,14],[5,11],[12,13],[8,11],[5,8],[5,10],[3,12],[5,9],[10,14],[13,14],[10,15],[1,2],[9,11],[2,5],[12,14],[1,2],[8,11],[0,12],[6,13],[4,8],[2,3],[5,11],[14,15],[0,9],[1,5],[4,15],[4,5],[0,10],[9,13]],[[6,11],[2,9],[2,15],[0,3],[8,11],[12,14],[0,3],[1,14],[3,12],[8,11],[3,6],[9,13],[7,9],[2,10],[10,12],[4,5],[9,15],[1,13],[2,11],[2,12],[0,13],[2,9],[10,15],[12,14],[1,4],[4,14],[10,12],[9,12],[6,10],[1,2],[6,9],[2,11],[1,6],[1,8],[0,3],[7,15],[7,9],[4,12],[10,12],[5,13],[5,7],[5,9],[8,12],[1,12],[13,14],[4,15],[0,7],[7,8],[3,6],[5,14],[5,15],[1,13],[7,8],[10,11],[0,9],[8,13],[12,15],[6,10],[10,15],[7,10],[1,13],[10,15],[9,15],[13,14],[8,12],[1,14],[4,11],[2,13],[8,13],[9,11],[3,9],[9,12],[2,5],[0,5],[3,4],[2,3],[7,12],[0,12],[8,14],[4,10],[5,8],[2,13],[4,11],[0,2],[8,13],[2,12],[5,12],[1,12],[3,5],[5,7],[7,14],[8,12],[5,13],[2,8],[2,6],[7,11],[1,3],[1,7],[0,10],[12,14],[7,11],[5,9],[9,10],[9,15],[1,10],[5,7],[5,11],[10,12],[4,15],[9,15],[2,8],[3,6],[2,6],[6,15],[7,12],[7,11],[6,7],[2,3],[6,11],[6,11],[9,14],[2,7],[10,13],[8,10],[7,10],[9,14],[1,15],[11,14],[12,14],[3,10],[0,2],[6,9],[0,7],[0,15],[1,14],[7,9],[1,2],[6,10],[0,7],[8,12],[6,7],[3,10],[4,9],[3,7],[4,5],[6,13],[6,12],[2,13],[4,11],[1,3],[5,6],[7,9],[6,15],[0,11],[12,13],[5,15],[1,9],[4,11],[2,14],[4,15],[4,6],[4,10],[2,10],[0,4],[7,11],[10,15],[5,6],[8,13],[3,11],[9,12],[3,12],[8,9],[6,10],[0,10],[4,10],[3,14],[0,5],[1,4],[3,11],[6,11],[2,7],[4,7],[6,10],[5,9],[7,13],[7,13],[0,4],[7,10],[1,13],[3,13],[3,7],[1,3],[2,15],[11,13],[5,14],[2,7],[4,13],[3,13],[2,14],[10,11],[5,14],[10,15],[3,6],[0,12],[6,15],[6,8],[3,11],[2,13],[2,3],[0,1],[1,14],[3,8],[5,12],[0,10],[9,14],[5,7],[9,10],[7,8],[6,11],[8,15],[6,14],[7,11],[13,14],[6,14],[2,6],[5,12],[0,15],[4,11],[1,9],[4,7],[8,15],[5,9],[7,13],[4,11],[1,3],[13,15],[5,14],[2,6],[6,8],[7,8],[0,5],[10,11],[7,13],[3,4],[3,9],[11,13],[10,11],[10,11],[0,15],[10,12],[7,14],[3,4],[3,12],[3,11],[3,10],[3,12],[8,10],[3,6],[0,14],[5,10],[4,7],[9,14],[0,10],[0,3],[7,15],[2,7],[1,3],[4,7],[8,12],[5,13],[13,15],[8,10],[0,12],[6,11],[8,12],[3,15],[2,13],[8,15],[8,11],[7,9],[4,8],[4,15],[5,9],[1,9],[1,9],[6,8],[0,15],[4,13],[1,9],[4,12],[0,15],[1,9],[1,2],[2,7],[10,11],[12,13],[10,15],[0,13],[3,6],[4,14],[11,12],[0,6],[1,4],[0,6],[9,15],[5,9],[0,9],[9,10],[4,14],[0,7],[11,14],[0,1],[1,8],[9,10],[1,15],[5,11],[1,15],[2,15],[8,12],[0,8],[12,15],[0,10],[1,11],[3,11],[2,4],[1,13],[0,8],[4,6],[6,14],[5,8],[5,10],[10,11],[5,9],[6,15],[8,13],[6,8],[9,11],[1,5],[2,4],[4,11],[10,11],[8,9],[2,10],[7,13],[0,4],[1,14],[7,8],[0,9],[9,13],[6,11],[0,12],[11,12],[9,14],[0,12],[3,4],[8,13],[3,15],[12,15],[1,4],[0,10],[0,6],[9,10],[5,9],[3,7],[6,7],[1,14],[1,3],[7,8],[6,12],[1,9],[1,2],[2,15],[10,15],[1,12],[9,10],[3,4],[3,8],[2,5],[9,14],[7,13],[7,10],[6,11],[2,7],[7,9],[4,11],[12,14],[1,6],[2,3],[1,15],[2,14],[5,9],[4,5],[4,13],[4,12],[6,8],[8,11],[8,12],[6,15],[9,14],[2,3],[2,15],[13,14],[5,9],[2,12],[4,8],[14,15],[3,6],[7,12],[0,13],[11,15],[5,15],[0,11],[2,12],[3,15],[2,9],[4,5],[3,8],[6,14],[2,3],[5,12],[2,4],[5,14],[1,7],[0,11],[2,3],[2,10],[1,12],[11,15],[7,12],[4,9],[6,15],[1,3],[0,2],[11,12],[0,10],[0,15],[5,15],[4,15],[0,10],[0,4],[4,5],[3,8],[3,15],[1,6],[1,3],[5,11],[8,9],[1,14],[1,2],[6,7],[10,15],[0,3],[5,12],[0,11],[2,10],[6,9],[2,9],[4,11],[2,10],[6,9],[10,11],[3,12],[7,12],[2,9],[1,11],[8,14],[7,14],[7,10],[0,8],[4,14],[1,10],[0,4],[0,1],[11,15],[14,15],[0,8],[5,13],[10,12],[8,10],[3,12],[5,13],[9,15],[6,11],[4,13],[1,8],[7,14],[2,10],[6,14],[4,11],[0,12],[5,12],[0,13],[2,9],[3,15],[2,9],[8,9],[0,9],[2,15],[3,10],[0,14],[8,9],[4,15],[7,12],[8,15],[0,6],[2,5],[3,7],[11,13],[0,1],[1,10],[4,11],[3,15]],[[0,7],[14,15],[1,10],[8,14],[4,9],[3,5],[7,12],[10,13],[0,2],[3,8],[6,12],[3,11],[5,13],[7,10],[10,11],[2,8],[3,7],[1,2],[3,13],[9,10],[3,15],[0,1],[9,10],[6,14],[8,13],[6,7],[10,11],[3,14],[1,2],[7,8],[4,14],[2,10],[9,11],[4,14],[10,14],[5,9],[4,10],[1,3],[3,4],[1,7],[12,15],[1,11],[8,14],[2,8],[0,14],[0,2],[3,9],[11,13],[6,14],[12,15],[4,13],[5,14],[10,13],[7,9],[12,13],[4,12],[0,6],[2,8],[6,13],[0,7],[5,15],[0,8],[5,12],[9,11],[2,3],[6,14],[12,14],[0,11],[3,6],[3,12],[7,15],[1,6],[8,15],[0,2],[11,14],[5,9],[9,11],[2,11],[11,15],[0,14],[9,15],[1,2],[10,13],[5,14],[2,9],[0,8],[3,8],[5,7],[0,1],[5,15],[9,10],[10,12],[6,7],[6,11],[9,14],[1,15],[4,11],[12,15],[9,14],[6,13],[6,15],[2,12],[9,14],[5,12],[1,10],[6,9],[8,9],[5,13],[13,14],[6,13],[3,11],[0,14],[1,8],[11,14],[9,12],[4,10],[2,14],[7,9],[5,10],[1,2],[7,14],[7,11],[1,5],[0,5],[6,8],[8,11],[8,10],[12,14],[4,13],[8,10],[2,6],[10,15],[0,6],[6,13],[8,15],[8,14],[8,10],[2,14],[2,10],[0,6],[8,14],[5,6],[5,8],[11,15],[2,13],[3,13],[0,15],[2,13],[2,3],[0,7],[4,10],[1,9],[12,14],[0,11],[1,3],[6,12],[2,6],[2,5],[10,11],[1,5],[11,14],[0,8],[2,15],[10,15],[1,13],[4,15],[2,5],[1,12],[0,15],[7,12],[1,6],[0,14],[7,14],[3,8],[4,14],[6,12],[5,11],[0,9],[1,6],[4,15],[3,8],[2,13],[10,12],[8,15],[6,13],[3,5],[10,12],[7,15],[5,6],[1,3],[6,11],[2,15],[10,14],[0,5],[4,14],[5,12],[2,7],[12,13],[5,10],[3,12],[8,10],[2,6],[8,9],[4,12],[1,14],[8,9],[6,11],[3,14],[10,14],[0,4],[4,8],[4,6],[3,8],[4,5],[5,12],[3,15],[3,8],[0,12],[1,4],[0,11],[2,7],[4,9],[5,10],[12,14],[5,13],[5,8],[7,12],[13,14],[5,15],[14,15],[10,14],[2,3],[4,15],[5,9],[10,13],[0,15],[9,13],[0,8],[4,14],[4,10],[12,13],[4,5],[0,7],[4,8],[10,15],[7,10],[4,13],[11,14],[0,14],[9,15],[9,15],[0,7],[11,13],[8,14],[4,8],[2,7],[6,8],[11,12],[4,8],[5,15],[4,10],[0,15],[3,5],[1,5],[2,7],[2,15],[1,6],[1,10],[8,10],[14,15],[2,11],[8,10],[2,5],[3,14],[4,11],[1,13],[2,10],[5,12],[7,11],[10,13],[4,10],[2,4],[0,15],[3,9],[1,12],[1,9],[0,9],[11,12],[9,13],[10,12],[6,7],[1,2],[0,15],[1,2],[1,12],[8,15],[6,11],[5,6],[3,10],[1,9],[6,12],[13,15],[5,15],[2,9],[0,7],[2,10],[9,11],[5,15],[5,11],[0,11],[3,13],[9,14],[11,15],[1,6],[0,3],[2,14],[4,15],[3,7],[9,13],[1,11],[2,11],[1,8],[0,12],[0,11],[0,2],[2,4],[2,14],[7,15],[7,10],[1,10],[3,7],[9,10],[6,8],[6,12],[3,4],[4,11],[10,12],[0,9],[4,15],[2,4],[5,15],[2,7],[4,11],[2,3],[9,15],[10,15],[6,11],[0,3],[7,10],[3,12],[5,11],[2,8],[4,6],[4,14],[6,13],[2,9],[1,14],[11,12],[0,11],[3,10],[5,10],[8,10],[1,7],[1,7],[7,11],[9,10],[7,11],[5,8],[3,4],[1,13],[6,7],[5,9],[2,3],[2,3],[7,11],[10,13],[0,15],[7,8],[5,8],[0,14],[11,14],[2,15],[6,12],[10,11],[10,13],[0,2],[1,4],[8,12],[5,8],[4,12],[3,8],[7,9],[8,12],[0,14],[11,12],[10,12],[7,13],[1,9],[2,15],[4,8],[1,14],[2,12],[3,9],[9,12],[11,15],[6,12],[10,12],[6,15],[9,10],[10,15],[6,7],[0,11],[4,8],[14,15],[6,11],[3,11],[6,13],[9,15],[12,13],[2,15],[9,10],[1,14],[0,6],[4,15],[3,15],[1,14],[3,6],[0,1],[0,4],[1,13],[11,13],[4,7],[10,11],[4,13],[11,15],[9,13],[1,12],[3,5],[0,11],[7,12],[1,14],[1,7],[0,1],[0,8],[4,9],[6,13],[4,10],[1,14],[10,15],[9,14],[5,13],[0,15],[0,8],[2,8],[9,14],[2,4],[4,9],[0,11],[3,11],[4,5],[3,9],[3,11],[6,15],[1,15],[2,8],[1,14],[9,14],[7,13],[2,7],[4,6],[8,13],[4,12],[1,12],[4,8],[1,2],[7,12],[1,9],[2,5],[5,7],[1,12],[6,8],[1,7],[4,7],[4,7],[9,11],[0,12],[3,13],[0,4],[4,6],[7,15],[1,10],[12,13],[1,2],[12,14],[0,11],[1,3],[2,3],[6,7],[2,10],[5,8],[1,13],[6,7],[0,5],[4,9],[4,5],[6,12],[12,14],[0,4],[12,13],[11,15],[6,15],[1,14]],[[0,14],[5,8],[6,15],[0,13],[0,15],[0,14],[1,7],[2,3],[3,13],[3,7],[0,6],[3,13],[8,13],[10,15],[1,11],[4,11],[2,10],[13,14],[13,14],[7,14],[4,10],[1,9],[3,12],[5,14],[0,8],[5,13],[0,7],[0,15],[7,13],[6,13],[3,10],[5,11],[0,4],[1,13],[13,14],[0,11],[0,10],[7,14],[0,15],[0,9],[10,14],[8,12],[5,10],[8,14],[4,6],[0,10],[7,15],[4,15],[8,11],[8,10],[8,15],[5,13],[1,3],[7,15],[7,9],[8,11],[3,13],[0,2],[10,12],[3,5],[5,7],[12,15],[2,14],[14,15],[7,14],[5,15],[6,12],[5,7],[3,11],[3,8],[0,12],[8,10],[1,10],[0,3],[12,15],[6,10],[2,8],[4,14],[12,15],[1,11],[1,7],[2,9],[1,5],[7,13],[0,11],[14,15],[1,9],[2,5],[2,15],[5,13],[7,15],[14,15],[2,3],[0,2],[10,12],[3,9],[12,13],[7,9],[7,12],[6,9],[3,14],[11,13],[2,13],[2,14],[6,8],[5,14],[8,10],[8,14],[5,8],[11,14],[3,5],[6,11],[2,3],[0,13],[4,15],[8,9],[11,13],[5,12],[2,10],[6,11],[2,7],[1,5],[3,5],[3,11],[5,14],[12,15],[11,12],[0,1],[9,13],[2,11],[13,14],[10,11],[4,15],[0,2],[2,5],[1,8],[1,2],[4,15],[9,15],[10,13],[12,14],[3,9],[6,13],[3,9],[6,15],[1,3],[3,4],[0,9],[4,11],[11,14],[3,14],[7,10],[1,10],[5,7],[2,8],[8,12],[11,13],[1,6],[4,15],[9,14],[1,14],[3,11],[0,10],[0,4],[6,8],[1,15],[6,12],[5,15],[2,8],[3,14],[2,5],[0,4],[3,13],[4,5],[7,14],[3,13],[7,14],[1,8],[1,6],[6,13],[4,13],[2,11],[2,14],[3,12],[4,13],[5,13],[1,4],[4,5],[3,13],[0,11],[2,3],[0,8],[0,4],[2,3],[2,11],[0,10],[5,11],[12,13],[3,13],[10,13],[5,6],[10,12],[4,8],[1,15],[3,4],[3,5],[8,11],[7,9],[6,15],[0,14],[8,9],[4,11],[9,15],[3,12],[8,9],[9,14],[11,15],[3,14],[3,9],[4,5],[10,11],[2,4],[13,14],[1,9],[1,6],[3,5],[3,4],[2,6],[8,13],[3,8],[8,12],[10,15],[6,14],[5,8],[0,14],[13,14],[0,13],[7,11],[1,12],[7,12],[2,6],[10,13],[3,11],[3,13],[2,11],[0,2],[3,6],[6,14],[2,11],[4,15],[6,9],[11,15],[7,11],[5,11],[5,15],[3,9],[9,10],[3,11],[1,12],[11,15],[1,5],[0,10],[0,12],[4,9],[4,7],[5,13],[10,12],[4,10],[4,11],[9,10],[10,12],[3,7],[4,6],[4,6],[7,8],[2,7],[0,7],[6,13],[7,12],[0,1],[2,7],[5,15],[5,13],[2,11],[1,5],[0,10],[6,13],[0,6],[1,7],[0,12],[10,11],[3,12],[2,12],[9,11],[4,13],[2,14],[4,12],[9,10],[0,6],[7,14],[8,12],[4,10],[8,10],[2,5],[2,15],[8,14],[4,10],[7,8],[13,15],[0,9],[1,12],[5,12],[3,10],[9,10],[4,14],[2,12],[4,5],[10,12],[10,14],[1,6],[5,14],[13,14],[7,14],[10,13],[5,13],[7,11],[4,12],[4,8],[3,6],[0,10],[1,15],[9,14],[6,7],[7,9],[4,11],[4,15],[10,15],[5,9],[4,5],[3,4],[7,8],[11,12],[2,14],[5,14],[0,12],[3,14],[1,2],[1,8],[12,13],[4,10],[5,10],[0,12],[9,11],[0,5],[9,14],[7,11],[6,10],[5,7],[1,3],[3,4],[4,12],[2,13],[2,7],[2,7],[4,15],[10,11],[6,10],[5,12],[11,12],[3,12],[8,15],[2,10],[11,13],[0,6],[0,13],[6,7],[7,10],[2,3],[3,9],[11,12],[12,14],[2,13],[6,15],[10,14],[3,10],[2,5],[2,13],[7,9],[5,15],[9,14],[7,12],[6,12],[9,13],[2,11],[0,6],[4,14],[12,14],[1,2],[1,5],[9,11],[12,13],[9,12],[1,12],[4,13],[10,14],[5,7],[1,9],[0,11],[2,7],[10,12],[1,11],[6,9],[7,15],[1,14],[5,11],[4,7],[9,15],[0,8],[3,11],[8,11],[7,9],[4,15],[0,7],[7,8],[5,7],[5,11],[0,11],[1,7],[2,15],[2,8],[5,10],[1,10],[3,6],[1,3],[2,5],[4,6],[4,15],[5,6],[7,15],[13,14],[4,7],[1,12],[10,15],[1,8],[3,12],[1,15],[1,6],[2,9],[0,14],[9,11],[2,15],[0,9],[3,4],[4,7],[3,10],[1,2],[4,5],[2,14],[11,15],[8,12],[3,8],[5,10],[4,12],[7,8],[0,10],[5,10],[0,9],[0,8],[0,5],[6,10],[9,15],[3,5],[11,13],[10,15],[8,12],[5,6],[10,14],[9,12],[7,13],[1,12],[7,11],[10,11],[4,15],[4,12],[0,13],[7,12],[1,10],[4,15],[7,10],[2,3],[5,9],[13,15],[9,14],[1,5],[7,13],[12,15],[7,11],[8,13],[1,14],[8,15],[9,15],[1,10],[9,14],[4,14],[8,13],[8,11],[2,3],[1,5],[4,13],[4,7],[9,12],[5,13]],[[7,9],[0,8],[2,10],[1,13],[1,11],[0,4],[8,12],[7,14],[10,12],[0,7],[0,14],[3,12],[4,13],[11,14],[6,7],[4,12],[1,2],[11,13],[0,4],[9,13],[0,15],[0,11],[5,14],[9,12],[12,15],[1,3],[4,6],[10,14],[3,5],[3,8],[2,10],[2,7],[3,6],[10,12],[2,7],[6,14],[4,8],[3,9],[3,8],[4,9],[4,12],[1,15],[10,13],[4,14],[9,12],[4,15],[5,9],[7,15],[13,14],[3,4],[1,4],[3,5],[2,4],[13,15],[11,15],[3,11],[8,14],[7,9],[0,15],[2,13],[6,14],[1,4],[11,14],[7,15],[2,12],[7,15],[0,12],[11,14],[4,10],[7,11],[1,3],[2,11],[0,5],[1,3],[1,8],[0,11],[5,11],[3,6],[3,15],[4,14],[0,9],[9,11],[1,15],[3,6],[0,10],[6,9],[4,10],[5,13],[4,14],[13,14],[10,12],[6,9],[7,12],[12,13],[7,13],[8,9],[10,12],[6,14],[12,15],[11,13],[6,8],[1,9],[6,15],[10,11],[1,5],[11,12],[2,5],[1,9],[8,12],[10,14],[5,10],[2,12],[14,15],[7,10],[2,10],[0,7],[5,12],[9,11],[11,12],[0,5],[11,13],[14,15],[1,10],[4,6],[8,15],[2,5],[10,15],[12,15],[4,5],[0,15],[2,14],[10,12],[4,11],[8,14],[0,3],[7,13],[4,10],[11,13],[1,6],[7,9],[5,11],[4,12],[2,6],[9,12],[8,15],[1,6],[4,14],[6,10],[9,14],[8,13],[7,12],[0,5],[0,6],[3,11],[13,14],[3,14],[0,5],[14,15],[0,15],[1,6],[8,14],[2,4],[2,15],[9,13],[7,15],[0,3],[14,15],[4,13],[2,13],[3,10],[11,14],[0,2],[7,15],[2,12],[10,12],[1,4],[2,8],[13,14],[2,6],[1,7],[3,6],[6,8],[11,15],[2,3],[2,9],[1,9],[0,10],[3,8],[4,10],[5,15],[13,14],[0,2],[1,5],[0,13],[6,10],[4,11],[6,13],[1,12],[7,15],[2,8],[0,1],[6,7],[3,6],[0,12],[0,13],[0,7],[0,6],[1,4],[2,12],[4,11],[0,15],[2,9],[10,12],[0,4],[3,6],[3,8],[1,7],[7,15],[0,13],[5,11],[8,13],[6,14],[1,13],[4,13],[2,10],[8,10],[4,8],[10,13],[8,15],[3,8],[3,11],[1,7],[1,6],[5,6],[5,10],[13,15],[2,4],[3,7],[4,14],[13,15],[0,2],[8,14],[8,11],[0,6],[8,14],[7,15],[7,15],[5,9],[5,14],[10,13],[1,12],[10,15],[6,10],[0,9],[3,11],[12,15],[0,2],[0,4],[1,10],[6,9],[3,5],[6,10],[2,3],[6,14],[1,9],[8,14],[9,10],[4,11],[4,15],[3,8],[12,15],[3,14],[3,5],[6,14],[3,7],[3,9],[1,2],[9,11],[4,9],[13,14],[1,5],[0,7],[0,13],[0,13],[1,4],[1,13],[5,12],[2,9],[2,7],[2,11],[9,14],[8,13],[8,14],[8,12],[7,13],[10,14],[0,15],[1,7],[1,6],[6,14],[2,13],[3,4],[7,10],[1,11],[9,15],[0,8],[1,2],[2,8],[12,15],[0,13],[1,6],[9,13],[3,14],[2,5],[8,13],[8,10],[7,12],[0,13],[5,13],[5,8],[10,11],[2,12],[4,5],[2,7],[1,12],[5,14],[3,12],[7,15],[2,11],[3,7],[9,11],[14,15],[7,15],[0,4],[4,5],[8,14],[9,14],[1,5],[2,12],[0,3],[2,4],[0,11],[10,15],[0,3],[0,5],[10,13],[1,7],[7,9],[8,12],[3,4],[8,13],[0,11],[3,13],[5,10],[1,9],[4,9],[0,2],[10,14],[1,7],[8,11],[2,9],[10,11],[5,14],[7,10],[1,13],[6,7],[4,12],[4,5],[0,3],[2,14],[8,14],[5,14],[6,12],[9,14],[2,13],[3,13],[2,5],[3,12],[10,15],[9,13],[0,4],[6,11],[5,10],[1,15],[6,15],[5,15],[7,10],[5,10],[1,4],[2,9],[4,8],[2,14],[3,10],[6,12],[9,11],[0,9],[2,11],[9,14],[1,8],[1,9],[1,3],[4,5],[5,8],[8,10],[0,8],[8,10],[2,5],[5,15],[5,8],[12,14],[11,14],[8,14],[14,15],[7,14],[5,11],[1,8],[4,8],[10,15],[3,11],[2,10],[1,6],[5,11],[1,2],[12,15],[5,14],[12,14],[7,15],[9,13],[5,6],[1,9],[0,8],[5,8],[8,11],[4,5],[8,9],[0,4],[1,7],[5,6],[11,12],[0,4],[0,1],[1,8],[1,9],[14,15],[11,14],[10,15],[10,15],[5,7],[6,8],[3,10],[3,7],[1,9],[1,7],[7,13],[0,8],[2,9],[4,12],[4,15],[1,12],[2,6],[2,6],[3,10],[1,4],[2,13],[2,4],[5,6],[5,12],[0,8],[1,9],[3,5],[4,8],[0,4],[5,6],[6,8],[10,11],[0,6],[1,14],[8,13],[4,10],[0,7],[10,14],[2,15],[1,4],[4,7],[2,9],[11,14],[2,9],[4,6],[12,13],[6,8],[5,6],[8,15],[6,10],[3,13],[3,7],[1,4],[3,12],[7,8],[1,5],[0,5],[3,11],[8,12],[0,15],[2,11],[4,11],[8,10],[5,13],[4,15],[4,15],[7,11],[1,5],[8,15]],[[6,12],[5,9],[1,10],[0,8],[7,8],[8,12],[5,13],[9,11],[1,12],[0,9],[0,2],[2,6],[11,15],[14,15],[5,8],[8,12],[7,10],[7,14],[0,12],[1,13],[3,7],[2,12],[9,12],[1,2],[1,10],[1,10],[9,15],[1,9],[1,15],[1,8],[10,14],[7,13],[2,15],[3,13],[8,13],[1,15],[7,10],[5,9],[7,9],[10,13],[4,11],[3,9],[0,1],[3,10],[0,4],[11,14],[1,11],[3,13],[5,6],[6,13],[6,13],[1,4],[8,14],[7,10],[1,5],[10,14],[4,8],[3,11],[12,15],[8,9],[11,14],[7,12],[0,8],[3,12],[2,13],[9,14],[5,12],[0,9],[7,10],[3,13],[9,12],[10,14],[8,9],[1,10],[1,3],[6,14],[1,5],[0,3],[11,13],[2,14],[4,13],[4,9],[1,7],[5,7],[0,7],[4,12],[6,9],[2,4],[6,8],[5,14],[2,11],[8,9],[1,2],[1,15],[6,11],[1,10],[9,13],[3,7],[0,4],[7,12],[3,11],[10,11],[4,6],[5,6],[5,9],[4,7],[5,10],[3,9],[4,7],[11,15],[1,8],[7,9],[5,8],[0,11],[7,14],[1,5],[6,12],[2,7],[4,8],[4,12],[4,11],[5,6],[6,8],[6,12],[0,5],[6,7],[8,10],[4,12],[9,14],[7,8],[0,5],[2,6],[5,15],[6,9],[1,13],[11,12],[6,9],[6,12],[4,10],[1,4],[3,7],[8,10],[6,7],[13,15],[0,1],[6,14],[6,9],[9,14],[11,13],[6,12],[12,13],[7,15],[4,10],[8,9],[5,11],[4,5],[9,15],[9,14],[11,12],[7,14],[1,6],[1,12],[2,9],[11,13],[6,15],[2,7],[1,3],[2,12],[4,7],[12,15],[3,9],[1,3],[4,8],[7,12],[4,9],[0,11],[0,1],[7,10],[0,13],[1,5],[4,7],[11,15],[0,8],[1,14],[3,14],[0,7],[0,6],[5,14],[3,9],[0,4],[1,2],[4,12],[3,14],[13,15],[6,10],[9,11],[0,15],[0,9],[7,9],[3,4],[2,12],[5,12],[1,13],[4,14],[2,3],[12,13],[4,8],[1,7],[9,15],[3,10],[2,4],[2,15],[0,9],[10,12],[4,15],[11,15],[3,8],[6,8],[1,8],[3,12],[5,12],[4,12],[0,2],[0,3],[5,12],[0,8],[2,10],[4,15],[4,5],[3,11],[12,13],[3,13],[4,13],[9,14],[6,15],[6,12],[7,12],[7,14],[7,9],[1,7],[0,5],[6,7],[10,11],[4,10],[3,11],[4,6],[3,14],[8,15],[2,4],[1,12],[8,9],[6,14],[1,3],[6,12],[0,6],[8,9],[5,8],[3,4],[5,8],[4,10],[0,8],[11,15],[0,11],[5,9],[3,6],[0,6],[2,13],[12,15],[9,13],[0,9],[10,13],[1,2],[3,13],[3,8],[11,14],[3,13],[13,14],[1,4],[1,15],[1,8],[5,8],[1,2],[3,10],[7,10],[5,15],[1,10],[1,14],[6,7],[1,7],[12,13],[3,12],[3,9],[8,9],[1,15],[7,15],[1,12],[2,9],[8,15],[9,14],[2,6],[5,7],[11,13],[9,15],[9,10],[4,13],[9,11],[0,5],[11,12],[0,8],[10,11],[3,11],[9,12],[11,13],[1,9],[4,13],[3,9],[0,2],[1,7],[0,7],[0,14],[3,6],[5,14],[9,15],[2,14],[4,5],[8,15],[0,12],[11,12],[0,12],[0,9],[1,6],[6,10],[0,15],[3,13],[8,15],[6,8],[3,14],[7,11],[0,13],[2,14],[1,6],[4,15],[2,9],[7,15],[2,10],[5,12],[9,10],[13,14],[6,15],[11,15],[14,15],[6,15],[11,13],[7,12],[11,15],[13,14],[2,10],[11,15],[2,15],[1,6],[1,5],[11,14],[0,8],[1,9],[5,10],[2,5],[0,12],[0,8],[3,12],[3,6],[12,15],[5,14],[4,5],[2,15],[12,15],[0,2],[7,14],[0,2],[9,11],[2,9],[4,5],[1,14],[8,15],[2,14],[10,14],[2,9],[1,15],[6,8],[0,3],[3,9],[3,12],[3,6],[0,13],[4,15],[9,13],[4,11],[12,15],[0,9],[0,9],[10,14],[5,7],[4,10],[8,12],[4,8],[8,11],[0,3],[6,12],[9,11],[4,5],[3,8],[1,5],[5,12],[13,15],[5,14],[12,13],[11,15],[2,12],[2,10],[2,8],[7,10],[5,13],[0,9],[3,14],[9,10],[6,14],[10,14],[0,12],[5,15],[2,9],[4,13],[0,15],[6,8],[5,12],[3,13],[4,14],[6,8],[6,10],[3,13],[1,9],[6,10],[2,3],[2,3],[2,15],[4,8],[7,11],[1,15],[1,8],[4,15],[8,9],[1,12],[1,6],[4,14],[12,14],[3,4],[3,13],[3,8],[8,15],[2,6],[12,15],[10,15],[10,14],[12,14],[11,14],[5,10],[4,7],[0,11],[5,14],[6,10],[0,11],[0,14],[13,14],[13,15],[7,13],[4,9],[7,14],[0,7],[2,5],[2,9],[8,14],[2,15],[1,2],[1,4],[4,9],[4,10],[1,9],[9,15],[3,15],[2,15],[4,13],[1,11],[3,4],[3,6],[8,9],[5,10],[8,15],[2,8],[8,9],[12,13],[0,9],[0,1],[5,11],[2,12],[13,14],[11,14],[11,12],[2,12],[11,15],[7,8],[5,11],[7,13],[5,13],[3,12]],[[6,15],[5,14],[7,12],[3,12],[6,8],[9,10],[8,10],[8,11],[3,15],[5,11],[7,11],[1,10],[12,13],[2,13],[11,13],[2,14],[1,6],[4,8],[1,13],[4,6],[9,14],[12,15],[14,15],[4,13],[3,14],[5,10],[3,10],[7,10],[1,15],[6,13],[1,7],[3,14],[2,14],[8,11],[6,7],[8,12],[8,15],[6,14],[0,6],[1,13],[2,5],[1,5],[4,9],[12,13],[9,10],[4,11],[3,6],[4,12],[0,7],[4,6],[5,7],[6,7],[3,12],[12,15],[3,4],[8,11],[3,11],[1,11],[4,14],[4,12],[8,10],[9,10],[7,8],[6,11],[1,4],[0,12],[3,10],[7,8],[0,8],[2,8],[2,5],[9,14],[7,8],[7,14],[10,13],[1,8],[5,15],[5,12],[3,10],[1,12],[3,9],[5,10],[1,6],[7,13],[0,1],[3,13],[1,3],[5,7],[0,14],[8,9],[4,7],[0,2],[1,8],[7,9],[3,15],[6,9],[5,14],[2,6],[12,13],[1,8],[6,13],[6,15],[2,10],[0,10],[2,13],[3,4],[4,15],[7,9],[9,11],[9,11],[10,14],[0,6],[9,15],[0,13],[8,10],[8,14],[4,15],[2,5],[2,14],[6,14],[3,11],[7,12],[0,7],[13,14],[5,7],[6,7],[5,6],[2,10],[1,7],[10,11],[7,14],[1,6],[4,9],[2,14],[1,15],[11,12],[11,13],[1,9],[1,12],[9,10],[8,13],[4,7],[0,1],[5,11],[5,13],[5,12],[3,9],[7,14],[2,7],[5,6],[5,9],[5,8],[4,7],[0,14],[4,11],[2,7],[6,13],[9,12],[0,10],[0,2],[2,6],[2,8],[6,8],[2,13],[0,8],[1,12],[11,12],[5,15],[6,7],[0,8],[5,13],[0,9],[5,9],[3,9],[4,6],[1,13],[2,10],[1,9],[3,14],[2,4],[10,12],[10,14],[0,10],[6,12],[6,13],[7,15],[1,10],[5,13],[6,15],[5,15],[1,9],[4,5],[2,8],[1,15],[9,10],[5,8],[9,12],[3,8],[0,13],[0,2],[9,14],[10,13],[2,11],[0,4],[7,11],[8,13],[2,14],[1,3],[1,2],[3,5],[0,4],[14,15],[1,14],[10,12],[3,5],[2,7],[11,12],[8,11],[5,10],[3,5],[5,15],[1,14],[7,13],[10,14],[5,9],[3,6],[9,13],[9,14],[1,10],[0,8],[9,13],[6,7],[5,14],[4,10],[8,13],[5,8],[11,13],[9,15],[4,13],[6,7],[0,12],[0,14],[0,1],[3,5],[9,13],[7,10],[5,11],[1,9],[0,8],[6,14],[2,11],[1,4],[0,2],[6,11],[2,11],[7,12],[2,8],[3,6],[1,6],[3,13],[7,14],[2,13],[1,3],[1,14],[4,5],[3,10],[5,14],[2,9],[2,7],[6,15],[4,15],[12,13],[2,14],[14,15],[0,2],[1,14],[1,7],[0,13],[9,12],[8,11],[6,11],[4,10],[0,5],[1,11],[1,13],[1,11],[4,5],[2,7],[2,7],[6,8],[9,11],[2,6],[9,14],[7,12],[11,13],[3,8],[1,5],[5,14],[3,10],[1,14],[1,7],[7,8],[2,7],[6,8],[3,9],[4,7],[6,10],[2,9],[0,8],[7,8],[2,10],[0,1],[0,13],[2,3],[6,13],[5,7],[5,12],[4,15],[8,9],[0,10],[5,6],[8,10],[2,14],[1,12],[8,12],[8,12],[4,7],[9,15],[0,13],[9,11],[11,14],[3,14],[8,15],[9,14],[0,13],[1,2],[0,9],[2,4],[4,9],[2,4],[8,11],[2,15],[3,8],[2,12],[10,14],[4,15],[7,10],[1,5],[7,9],[2,4],[1,13],[6,7],[2,14],[11,14],[2,5],[3,6],[6,7],[1,2],[6,15],[6,7],[4,12],[5,14],[10,13],[1,6],[0,1],[7,13],[6,15],[8,15],[8,9],[0,10],[1,7],[6,7],[2,10],[4,10],[12,15],[0,6],[9,15],[8,15],[6,11],[2,13],[10,13],[7,10],[3,11],[5,9],[0,11],[5,12],[6,13],[2,10],[2,7],[0,9],[3,6],[10,12],[0,5],[5,6],[6,9],[6,9],[4,8],[1,6],[12,14],[1,11],[3,14],[8,15],[3,13],[4,7],[10,14],[2,3],[4,10],[2,9],[11,14],[9,15],[9,14],[5,7],[0,2],[12,13],[12,13],[0,8],[0,12],[0,5],[0,5],[3,6],[8,14],[4,5],[11,12],[4,14],[9,14],[4,5],[11,12],[1,3],[1,13],[13,15],[7,11],[2,4],[8,13],[12,15],[7,14],[13,14],[3,8],[9,11],[6,13],[1,7],[1,10],[0,15],[3,15],[2,15],[3,4],[4,10],[10,13],[2,5],[5,13],[4,10],[4,6],[8,13],[3,14],[3,15],[3,12],[5,11],[5,11],[5,10],[3,9],[0,13],[10,11],[7,11],[8,9],[8,9],[5,9],[4,14],[4,13],[0,5],[7,9],[8,10],[11,15],[7,10],[0,3],[1,10],[2,13],[1,3],[4,15],[4,9],[0,6],[1,11],[8,11],[0,8],[7,15],[14,15],[0,9],[2,12],[1,2],[4,12],[3,4],[2,14],[6,8],[0,13],[9,12],[2,9],[8,12],[7,13],[9,15],[11,14],[12,15],[6,9],[10,15],[6,12],[5,9],[12,13],[8,11],[9,12],[5,8],[9,13],[5,7],[8,12],[10,13],[7,12]],[[2,13],[0,10],[5,15],[1,11],[1,4],[13,15],[2,4],[7,10],[3,12],[4,5],[0,12],[1,9],[10,11],[4,12],[11,15],[11,14],[11,12],[4,14],[1,3],[7,15],[5,10],[1,4],[4,8],[5,7],[4,14],[6,10],[1,12],[2,15],[11,15],[8,9],[1,3],[0,9],[0,1],[6,14],[0,1],[7,11],[2,6],[2,10],[1,8],[4,9],[10,15],[2,6],[10,14],[3,14],[1,15],[1,3],[8,9],[7,8],[4,5],[2,10],[5,11],[7,12],[0,14],[5,12],[10,11],[0,5],[9,15],[12,13],[5,11],[5,8],[3,4],[7,13],[0,6],[2,3],[3,9],[3,10],[3,6],[7,10],[6,11],[6,11],[0,8],[12,15],[10,14],[3,12],[3,5],[5,8],[1,14],[2,13],[3,12],[8,11],[1,3],[12,14],[3,10],[7,11],[7,15],[0,3],[1,6],[2,4],[9,12],[10,13],[0,7],[1,7],[5,15],[4,5],[5,15],[7,8],[1,12],[1,13],[5,11],[4,9],[3,9],[2,5],[2,8],[5,14],[0,9],[5,6],[3,13],[11,13],[7,10],[6,7],[0,8],[6,7],[1,4],[0,6],[8,10],[10,13],[3,4],[8,15],[4,7],[0,7],[2,13],[0,11],[11,14],[4,15],[3,9],[2,8],[0,5],[7,12],[5,15],[8,14],[6,15],[7,12],[9,14],[7,14],[6,13],[2,9],[2,4],[1,3],[1,8],[3,8],[12,13],[4,9],[11,13],[5,13],[2,7],[6,11],[4,12],[0,10],[9,13],[3,8],[3,6],[2,7],[0,8],[8,14],[8,9],[0,14],[7,15],[10,11],[2,7],[0,13],[11,12],[4,10],[12,14],[9,13],[12,14],[9,10],[0,2],[3,12],[4,5],[0,12],[4,13],[9,13],[0,9],[2,4],[7,10],[4,12],[8,14],[3,14],[3,13],[0,11],[6,12],[2,8],[11,13],[7,12],[8,13],[6,10],[3,13],[2,6],[3,8],[1,4],[1,9],[1,12],[0,6],[12,13],[3,11],[2,3],[3,4],[7,9],[3,4],[2,6],[8,9],[5,12],[4,7],[0,6],[2,3],[7,10],[6,7],[9,15],[8,13],[0,12],[3,5],[4,13],[1,13],[3,13],[7,14],[10,13],[3,9],[2,9],[7,10],[3,5],[5,11],[1,8],[3,13],[4,9],[10,15],[1,9],[1,10],[4,10],[7,15],[2,4],[6,12],[0,7],[1,10],[9,13],[9,15],[6,12],[2,10],[0,14],[3,15],[2,14],[7,12],[12,14],[4,8],[4,15],[10,15],[2,8],[3,7],[4,10],[8,10],[5,12],[5,14],[1,13],[9,13],[14,15],[12,13],[0,4],[3,12],[4,14],[0,3],[3,10],[1,5],[1,7],[7,10],[1,5],[4,14],[4,8],[4,10],[2,8],[1,11],[10,12],[8,9],[3,9],[0,6],[7,10],[4,14],[0,7],[1,4],[3,10],[2,12],[0,3],[6,7],[0,5],[9,10],[4,14],[0,1],[5,9],[5,7],[3,8],[1,8],[4,6],[3,10],[1,2],[0,7],[3,9],[11,13],[3,14],[5,6],[0,2],[8,13],[1,8],[2,15],[1,6],[6,15],[11,13],[13,14],[8,12],[5,8],[7,13],[3,13],[0,9],[3,8],[3,12],[6,7],[4,13],[2,12],[6,14],[4,12],[2,4],[1,5],[1,9],[11,12],[2,8],[3,4],[2,15],[10,15],[4,10],[5,7],[13,14],[0,8],[5,8],[8,10],[11,15],[2,6],[5,14],[11,13],[10,15],[3,5],[10,12],[3,4],[7,15],[0,8],[13,14],[12,14],[6,8],[0,9],[7,13],[2,7],[1,2],[4,10],[2,10],[2,7],[3,5],[6,9],[4,11],[8,10],[3,7],[0,9],[0,11],[1,11],[8,9],[4,7],[2,9],[8,12],[3,4],[3,9],[9,14],[3,14],[2,11],[2,8],[11,13],[1,2],[9,15],[9,13],[9,11],[12,14],[10,13],[1,9],[7,11],[2,11],[6,14],[1,5],[10,12],[5,9],[3,13],[1,7],[0,13],[6,13],[4,7],[4,5],[1,6],[13,14],[13,14],[2,4],[0,9],[8,15],[1,7],[5,15],[2,9],[4,5],[4,9],[0,15],[8,12],[0,11],[2,14],[3,9],[2,11],[8,13],[3,12],[4,10],[1,12],[3,8],[3,10],[1,3],[8,12],[4,12],[2,5],[8,9],[4,13],[5,13],[2,5],[3,15],[8,11],[2,11],[2,10],[4,6],[0,11],[1,13],[1,5],[0,7],[3,6],[1,10],[4,6],[2,5],[5,14],[3,11],[10,15],[6,11],[2,15],[3,15],[3,7],[11,14],[2,5],[4,7],[3,8],[2,15],[6,12],[7,14],[7,11],[1,12],[1,9],[2,15],[4,12],[4,10],[5,11],[5,9],[3,6],[3,9],[0,5],[4,10],[2,11],[6,7],[4,8],[7,9],[5,7],[0,7],[1,6],[1,4],[2,12],[0,11],[11,13],[13,15],[4,7],[1,9],[0,6],[2,14],[2,8],[6,7],[4,7],[0,14],[0,6],[1,10],[1,7],[6,13],[0,12],[4,13],[4,10],[2,9],[8,11],[3,9],[0,15],[7,9],[6,12],[14,15],[6,10],[6,15],[0,6],[3,6],[0,1],[1,10],[10,13],[2,10],[0,11],[0,1],[4,7],[4,7],[1,4],[2,9],[3,12],[12,13],[2,12],[11,13],[8,14]],[[8,14],[1,8],[3,10],[6,11],[12,15],[6,11],[1,2],[3,14],[2,11],[1,9],[9,10],[4,8],[0,4],[10,13],[0,9],[9,13],[2,3],[1,2],[4,8],[0,7],[11,14],[2,13],[8,12],[12,15],[10,14],[7,13],[1,12],[5,13],[3,9],[6,14],[4,10],[4,6],[5,8],[0,13],[0,12],[11,13],[3,11],[7,11],[5,12],[6,15],[0,6],[1,10],[2,4],[7,8],[5,10],[11,14],[9,10],[8,9],[7,13],[3,5],[6,15],[5,11],[12,15],[12,13],[0,11],[1,9],[7,9],[3,15],[6,15],[3,13],[3,12],[4,11],[8,11],[3,6],[3,5],[13,14],[0,9],[1,3],[0,9],[4,13],[3,15],[0,15],[8,15],[2,12],[1,2],[5,13],[7,13],[4,12],[3,5],[4,5],[1,7],[5,13],[4,7],[1,5],[5,6],[6,8],[0,4],[2,13],[0,3],[0,7],[8,14],[0,2],[8,9],[2,4],[10,15],[9,12],[11,12],[0,4],[6,15],[8,9],[1,3],[9,11],[1,9],[11,15],[7,14],[3,10],[0,5],[8,15],[1,5],[4,9],[2,4],[6,7],[8,10],[0,5],[11,15],[4,6],[12,15],[3,11],[3,6],[1,7],[3,11],[3,10],[8,12],[2,6],[8,11],[2,9],[1,2],[0,12],[8,10],[4,9],[9,15],[0,2],[2,5],[8,9],[2,7],[3,7],[4,5],[5,7],[11,14],[0,15],[3,15],[4,12],[2,9],[10,14],[8,14],[6,7],[8,15],[8,14],[0,5],[4,5],[0,10],[0,3],[0,5],[8,13],[6,8],[5,8],[3,11],[0,7],[1,4],[4,15],[6,9],[0,15],[12,15],[8,15],[1,11],[8,9],[7,9],[7,10],[14,15],[0,11],[2,4],[1,8],[1,11],[6,7],[4,12],[12,15],[6,13],[5,7],[1,5],[5,11],[6,13],[2,12],[0,4],[3,7],[1,10],[0,14],[11,12],[3,6],[6,11],[0,1],[0,9],[2,7],[1,3],[9,13],[0,2],[10,13],[12,13],[8,13],[2,7],[0,9],[3,8],[0,8],[2,10],[0,12],[0,8],[7,11],[4,13],[9,12],[0,13],[0,15],[1,10],[0,13],[5,9],[0,8],[9,11],[0,15],[4,15],[2,13],[0,15],[2,10],[6,7],[9,12],[2,10],[7,13],[2,15],[12,14],[6,8],[5,14],[12,13],[0,9],[2,6],[0,1],[5,11],[3,11],[5,10],[0,10],[3,14],[3,9],[4,14],[9,12],[9,11],[1,5],[12,15],[0,15],[2,7],[4,5],[1,6],[7,8],[2,6],[4,14],[4,15],[2,7],[1,12],[2,13],[0,13],[1,11],[7,12],[7,9],[1,2],[9,15],[7,14],[6,8],[7,15],[6,9],[8,11],[3,9],[9,15],[4,5],[1,13],[6,13],[1,5],[9,13],[2,14],[11,14],[5,7],[3,7],[0,4],[1,3],[7,13],[0,11],[0,3],[7,14],[4,9],[7,15],[4,14],[10,13],[8,10],[3,8],[3,7],[1,7],[10,11],[1,10],[0,14],[2,8],[2,6],[1,9],[3,15],[3,15],[3,14],[1,2],[4,12],[2,8],[0,12],[8,10],[7,14],[3,13],[11,13],[9,15],[10,13],[6,10],[1,5],[8,9],[7,11],[9,15],[14,15],[6,12],[1,13],[0,7],[5,9],[10,15],[2,10],[3,6],[4,5],[11,13],[10,13],[5,14],[0,6],[5,11],[6,14],[5,15],[3,4],[2,8],[9,15],[2,9],[2,5],[1,11],[12,14],[1,8],[11,12],[1,12],[0,7],[3,6],[9,10],[7,15],[2,7],[9,12],[1,10],[8,10],[3,12],[4,10],[2,13],[6,7],[3,12],[0,13],[6,8],[2,11],[0,10],[3,13],[8,15],[6,14],[6,14],[13,15],[1,9],[7,10],[2,10],[7,14],[0,6],[11,15],[5,13],[4,13],[4,12],[1,4],[6,8],[10,15],[13,14],[6,11],[4,14],[0,5],[8,13],[0,9],[11,14],[1,10],[10,11],[1,11],[11,13],[0,4],[13,15],[14,15],[8,15],[1,12],[5,13],[4,13],[2,13],[0,1],[3,7],[3,15],[6,13],[4,12],[6,7],[1,8],[9,14],[9,12],[0,11],[0,11],[12,15],[5,9],[9,15],[3,5],[0,8],[6,12],[4,14],[0,11],[1,7],[12,14],[7,14],[8,9],[8,10],[9,10],[10,13],[1,4],[1,9],[6,8],[5,14],[10,14],[8,13],[5,6],[9,13],[7,9],[1,15],[1,13],[1,9],[3,11],[3,9],[0,8],[8,15],[4,5],[5,6],[6,7],[0,3],[4,9],[7,12],[11,12],[5,10],[8,13],[3,14],[3,12],[9,11],[0,7],[4,10],[8,13],[6,15],[4,13],[0,8],[1,12],[0,5],[4,6],[8,15],[5,12],[12,13],[9,11],[8,9],[2,12],[8,15],[1,5],[1,4],[3,10],[13,15],[12,15],[5,12],[4,15],[2,5],[3,9],[13,15],[3,7],[4,13],[5,15],[1,15],[4,11],[3,5],[5,8],[7,12],[3,14],[7,15],[6,15],[12,15],[0,8],[11,15],[1,6],[9,11],[0,10],[0,13],[3,6],[1,10],[5,10],[2,11],[2,7],[0,9],[4,13],[8,14],[12,13],[3,4],[6,14],[0,9],[2,14],[0,13],[3,6],[1,3],[4,6],[0,6],[9,15],[0,11],[1,7]],[[7,12],[0,15],[6,14],[1,8],[8,11],[0,3],[9,15],[12,15],[3,10],[0,11],[13,15],[2,15],[3,10],[9,15],[3,13],[3,13],[0,7],[1,9],[1,7],[5,13],[8,11],[4,10],[4,7],[2,12],[6,14],[6,12],[10,11],[4,12],[2,9],[5,14],[3,6],[11,14],[13,15],[8,12],[6,7],[0,8],[1,3],[1,10],[5,11],[0,5],[2,3],[3,15],[5,6],[0,9],[12,14],[4,9],[7,9],[0,11],[5,7],[7,14],[12,15],[1,9],[5,12],[6,11],[9,13],[1,9],[1,5],[8,9],[0,3],[7,10],[3,13],[0,4],[5,10],[5,13],[5,14],[2,14],[9,10],[2,12],[10,13],[8,10],[1,7],[1,9],[5,12],[0,7],[6,14],[4,8],[5,7],[1,15],[7,12],[6,7],[2,10],[0,11],[2,7],[8,14],[0,9],[1,7],[9,14],[4,5],[6,13],[3,8],[2,8],[4,11],[0,9],[2,5],[2,3],[4,9],[3,8],[6,12],[10,12],[0,9],[3,9],[12,15],[9,11],[0,13],[3,15],[3,11],[5,12],[1,3],[4,13],[1,13],[7,11],[1,7],[3,8],[10,15],[1,3],[6,14],[1,10],[4,9],[3,9],[11,15],[5,11],[0,5],[6,13],[9,10],[1,14],[4,7],[7,11],[2,13],[6,8],[9,14],[2,13],[0,10],[0,7],[9,15],[11,12],[3,8],[0,9],[3,11],[4,8],[3,12],[5,9],[7,11],[13,15],[3,10],[2,7],[13,15],[7,8],[2,3],[5,12],[0,7],[0,15],[5,7],[6,10],[2,6],[0,4],[2,10],[7,9],[5,7],[3,4],[4,6],[3,9],[6,13],[0,10],[7,15],[1,5],[13,14],[9,13],[5,11],[1,4],[1,6],[4,8],[0,7],[0,15],[2,15],[8,15],[12,13],[0,14],[5,7],[1,9],[5,12],[8,13],[3,15],[0,13],[13,15],[7,14],[2,5],[1,8],[5,9],[0,1],[1,12],[2,5],[0,8],[9,11],[0,3],[6,14],[0,2],[0,13],[6,7],[3,5],[0,9],[0,7],[10,12],[1,4],[4,10],[0,9],[8,15],[2,9],[3,4],[1,10],[6,10],[7,15],[6,10],[4,14],[9,14],[0,15],[5,7],[1,14],[8,9],[0,1],[7,12],[3,4],[1,4],[3,13],[6,7],[12,14],[0,13],[10,14],[6,10],[2,11],[3,6],[1,9],[1,10],[5,14],[9,14],[8,10],[2,14],[1,10],[3,13],[0,8],[10,11],[6,15],[0,6],[8,13],[0,2],[5,6],[9,10],[9,14],[6,10],[3,14],[11,13],[6,13],[4,5],[3,10],[0,6],[8,11],[4,13],[3,11],[1,7],[7,9],[2,6],[7,10],[0,2],[4,11],[5,13],[5,12],[0,6],[11,15],[8,12],[0,13],[2,5],[8,9],[5,14],[11,14],[2,7],[12,14],[4,15],[5,12],[6,8],[9,11],[7,14],[3,6],[4,14],[0,3],[0,2],[12,13],[0,12],[6,8],[10,12],[2,6],[6,13],[10,14],[12,13],[0,6],[5,7],[5,15],[6,10],[3,11],[0,11],[3,15],[2,15],[10,13],[2,5],[6,11],[14,15],[0,5],[1,13],[8,13],[4,13],[5,12],[3,10],[1,14],[0,6],[3,11],[7,12],[9,10],[7,9],[2,11],[0,2],[0,4],[1,4],[11,14],[6,7],[8,10],[6,7],[3,8],[4,15],[0,12],[2,3],[9,13],[2,8],[9,10],[0,14],[8,12],[7,11],[8,11],[2,3],[5,9],[8,12],[9,14],[2,4],[5,7],[4,9],[6,7],[3,12],[7,9],[9,12],[9,15],[1,6],[11,13],[1,12],[9,12],[11,12],[9,15],[2,15],[8,9],[1,9],[3,13],[0,9],[8,15],[8,11],[2,15],[6,10],[7,10],[2,7],[1,11],[7,9],[8,9],[2,3],[0,5],[1,12],[3,9],[7,9],[6,12],[0,15],[2,11],[8,11],[8,10],[3,9],[6,9],[2,12],[7,9],[2,15],[0,7],[9,13],[10,12],[12,14],[2,7],[6,12],[5,15],[2,7],[11,15],[3,5],[7,15],[3,15],[1,9],[11,12],[1,3],[6,7],[6,8],[4,10],[10,15],[8,15],[14,15],[1,2],[3,8],[7,9],[1,2],[8,12],[7,9],[5,15],[1,15],[8,15],[5,12],[8,9],[4,7],[14,15],[1,3],[4,7],[0,15],[4,7],[8,15],[6,10],[5,6],[0,1],[6,9],[5,7],[13,15],[1,15],[9,12],[3,13],[9,15],[4,12],[10,11],[3,9],[3,8],[2,4],[6,13],[8,13],[3,4],[9,12],[12,15],[0,8],[1,15],[11,13],[6,8],[4,7],[0,10],[4,9],[1,2],[6,13],[0,8],[9,12],[9,12],[13,15],[9,12],[8,15],[3,6],[5,8],[0,2],[10,13],[3,12],[5,13],[4,12],[7,12],[1,12],[1,8],[1,13],[4,9],[5,14],[5,11],[6,14],[2,13],[0,1],[6,11],[2,8],[7,10],[8,12],[1,14],[2,6],[9,10],[7,15],[3,12],[5,10],[2,9],[1,8],[1,11],[4,13],[12,14],[2,9],[1,5],[2,4],[2,10],[7,9],[4,6],[9,14],[5,13],[1,15],[0,1],[1,9],[3,12],[12,14],[0,7],[7,13],[5,7],[2,6],[1,15],[8,9],[8,12],[0,10],[8,14],[4,12],[9,10]],[[3,8],[5,6],[0,15],[0,2],[3,6],[7,11],[2,6],[8,15],[5,11],[1,14],[6,11],[7,9],[2,11],[1,4],[1,9],[7,10],[6,12],[1,11],[0,12],[9,15],[2,4],[6,13],[1,7],[7,11],[2,10],[13,15],[12,13],[2,11],[7,12],[4,13],[2,5],[1,7],[1,6],[1,9],[5,11],[1,2],[1,2],[5,13],[2,5],[7,14],[7,11],[0,1],[4,15],[3,8],[9,13],[8,14],[8,11],[9,10],[6,15],[6,14],[13,14],[8,12],[10,13],[12,14],[9,10],[2,11],[5,6],[2,14],[8,11],[4,6],[0,6],[4,6],[4,15],[2,12],[5,8],[4,9],[5,8],[0,10],[0,10],[5,15],[4,7],[4,14],[1,8],[8,14],[6,11],[4,15],[4,10],[0,9],[8,15],[6,15],[8,13],[9,12],[9,13],[13,15],[3,4],[4,14],[9,11],[5,11],[5,9],[6,10],[14,15],[2,5],[9,12],[3,8],[0,10],[5,6],[3,7],[8,13],[2,11],[0,11],[6,13],[10,11],[0,2],[8,14],[5,7],[6,9],[4,14],[2,15],[3,13],[4,9],[6,12],[1,12],[8,13],[3,12],[2,4],[7,10],[5,14],[9,12],[4,6],[10,15],[1,4],[13,15],[8,12],[8,13],[1,8],[4,5],[7,15],[1,7],[1,14],[4,7],[7,8],[13,14],[2,5],[3,5],[3,12],[4,10],[3,12],[1,5],[6,9],[4,8],[4,14],[9,11],[9,11],[0,14],[5,11],[10,11],[3,14],[0,12],[5,8],[1,12],[6,14],[7,10],[4,15],[10,15],[10,11],[5,12],[5,14],[2,12],[5,7],[6,15],[8,9],[4,7],[0,2],[4,7],[9,12],[0,4],[3,15],[10,14],[4,15],[2,6],[2,6],[1,13],[4,8],[5,15],[3,5],[1,10],[1,14],[3,6],[1,14],[6,8],[11,13],[5,6],[2,5],[5,13],[2,5],[1,7],[10,12],[1,13],[13,15],[3,6],[2,5],[1,8],[5,12],[2,15],[9,13],[8,9],[7,9],[2,11],[4,12],[0,12],[5,10],[5,14],[4,13],[5,8],[0,10],[1,6],[6,8],[3,7],[3,5],[2,8],[9,11],[9,12],[3,9],[2,13],[2,4],[7,12],[2,3],[10,13],[13,14],[7,14],[1,10],[4,13],[11,14],[0,14],[2,3],[1,4],[4,15],[3,4],[11,14],[4,14],[8,13],[6,12],[0,4],[0,15],[2,10],[0,15],[1,3],[11,15],[4,15],[11,15],[13,14],[0,14],[3,13],[5,10],[2,4],[2,8],[6,14],[0,13],[0,7],[5,11],[8,12],[7,14],[4,9],[4,13],[0,9],[4,6],[1,11],[4,8],[9,11],[7,15],[3,5],[2,7],[0,1],[9,12],[5,9],[6,7],[5,11],[2,4],[6,10],[2,14],[1,10],[2,14],[1,14],[11,13],[2,4],[1,13],[0,9],[3,15],[0,3],[0,3],[7,13],[5,12],[2,5],[0,14],[0,2],[3,15],[3,7],[11,13],[0,8],[11,15],[5,8],[7,14],[2,12],[12,13],[2,10],[6,10],[1,15],[0,13],[4,7],[6,12],[0,12],[0,6],[4,6],[8,14],[12,13],[7,13],[13,14],[4,10],[2,6],[4,14],[6,9],[11,12],[7,12],[3,12],[8,9],[6,8],[6,8],[2,6],[13,15],[5,13],[4,6],[5,14],[2,9],[11,15],[4,8],[2,14],[10,15],[0,13],[4,15],[4,8],[12,15],[7,9],[5,15],[3,11],[2,9],[13,15],[1,9],[2,7],[3,8],[7,10],[3,5],[1,5],[8,14],[5,15],[4,9],[1,4],[7,12],[8,9],[6,7],[3,7],[11,15],[3,10],[2,12],[4,15],[6,15],[3,4],[3,14],[9,14],[6,12],[0,6],[12,14],[0,7],[7,11],[12,14],[5,6],[2,3],[0,7],[3,9],[11,14],[4,11],[9,13],[1,7],[5,8],[11,13],[1,15],[1,15],[3,9],[0,4],[0,7],[1,3],[11,15],[1,13],[5,14],[14,15],[0,4],[4,15],[0,11],[1,3],[6,11],[1,5],[12,15],[0,9],[7,9],[4,5],[8,13],[14,15],[4,11],[7,10],[8,13],[7,10],[1,3],[7,12],[4,15],[13,14],[2,3],[0,5],[1,9],[3,14],[5,6],[10,15],[0,13],[9,14],[0,9],[10,14],[6,13],[1,15],[12,15],[0,10],[4,7],[0,7],[3,8],[10,13],[9,11],[4,9],[5,15],[10,14],[6,7],[1,15],[11,14],[4,14],[5,8],[4,11],[1,9],[6,14],[6,8],[10,11],[3,15],[3,5],[1,4],[4,15],[12,15],[12,15],[12,15],[10,11],[2,4],[0,1],[6,10],[1,11],[6,13],[12,15],[6,14],[0,8],[6,10],[5,10],[8,11],[2,12],[11,13],[1,9],[6,8],[2,7],[13,14],[3,10],[8,10],[7,13],[2,12],[5,8],[0,9],[11,13],[10,11],[12,15],[1,2],[4,6],[12,14],[0,2],[3,11],[2,13],[2,4],[13,15],[12,14],[1,5],[4,13],[2,3],[1,8],[7,14],[5,14],[1,9],[1,2],[3,7],[6,11],[12,14],[7,15],[6,12],[0,11],[4,6],[8,14],[6,8],[4,8],[11,14],[1,3],[2,7],[8,12],[1,11],[0,11],[1,14],[8,15],[7,14],[2,14],[2,8],[2,14],[1,10],[0,13],[10,15]],[[6,8],[4,10],[1,6],[1,11],[0,15],[2,14],[9,14],[3,5],[3,14],[0,10],[14,15],[2,8],[2,10],[1,10],[4,14],[3,6],[2,14],[3,13],[9,11],[1,5],[1,11],[3,4],[5,14],[10,15],[11,13],[7,14],[1,2],[10,12],[6,7],[7,14],[7,13],[2,15],[3,14],[7,12],[1,8],[2,14],[0,3],[2,10],[6,9],[1,11],[3,9],[4,8],[11,14],[5,15],[2,7],[9,13],[0,14],[12,14],[3,14],[4,5],[8,14],[4,7],[11,14],[3,6],[5,15],[6,7],[3,8],[8,9],[6,15],[1,7],[5,13],[1,2],[1,6],[3,12],[2,12],[0,3],[3,10],[3,4],[14,15],[0,15],[3,10],[5,7],[0,15],[0,14],[0,7],[5,13],[6,12],[0,1],[0,8],[9,12],[3,4],[0,9],[0,13],[5,12],[8,10],[2,11],[4,8],[0,5],[2,10],[4,8],[4,10],[2,6],[6,12],[10,11],[12,15],[1,11],[3,14],[3,9],[3,13],[5,14],[2,10],[12,15],[0,11],[4,9],[4,5],[10,13],[8,10],[6,10],[3,15],[3,11],[4,7],[2,15],[0,15],[1,14],[4,6],[2,3],[2,14],[2,7],[7,10],[7,8],[0,10],[0,10],[6,13],[0,4],[4,15],[8,11],[0,7],[2,13],[1,13],[6,15],[3,7],[7,12],[8,10],[2,15],[2,3],[1,4],[3,14],[4,11],[1,3],[2,8],[7,11],[4,6],[8,15],[10,15],[9,15],[7,9],[10,12],[4,11],[1,10],[10,12],[7,12],[2,5],[5,10],[14,15],[7,14],[7,15],[5,15],[5,13],[8,11],[2,7],[7,13],[1,6],[3,4],[11,13],[2,8],[3,6],[13,14],[9,11],[1,12],[3,14],[2,15],[1,3],[3,10],[7,12],[4,10],[2,8],[13,15],[5,12],[12,15],[1,5],[0,12],[11,14],[8,15],[1,8],[2,12],[5,8],[11,15],[9,15],[4,12],[6,15],[11,14],[2,8],[4,6],[7,13],[11,13],[8,14],[8,12],[2,13],[4,9],[3,8],[0,13],[2,14],[0,7],[2,4],[3,10],[7,12],[6,14],[2,5],[10,12],[5,8],[3,7],[10,11],[3,4],[2,15],[6,10],[5,11],[8,10],[0,6],[0,13],[12,15],[2,11],[1,9],[0,1],[9,15],[3,11],[4,13],[10,11],[3,4],[3,15],[5,7],[5,14],[1,15],[5,14],[7,11],[11,14],[1,10],[2,13],[4,13],[10,13],[5,6],[4,7],[9,13],[2,12],[9,15],[7,13],[0,12],[5,13],[7,11],[2,15],[4,14],[5,13],[9,11],[4,12],[12,13],[5,15],[10,11],[10,13],[2,13],[1,4],[7,14],[0,3],[4,5],[4,15],[6,11],[7,8],[5,11],[4,8],[5,12],[0,6],[13,15],[1,14],[14,15],[1,9],[1,12],[3,4],[2,10],[7,14],[1,5],[1,7],[1,15],[5,6],[0,11],[3,9],[5,9],[8,9],[3,9],[0,1],[6,8],[3,7],[0,3],[3,13],[2,8],[0,5],[2,12],[7,11],[0,11],[9,15],[10,11],[1,7],[2,10],[0,10],[1,13],[7,12],[0,11],[0,6],[3,13],[3,8],[11,13],[2,15],[4,13],[2,9],[3,10],[3,10],[2,7],[0,10],[1,14],[11,14],[2,9],[7,13],[7,11],[0,11],[9,12],[0,2],[1,14],[2,7],[4,6],[1,5],[11,12],[2,8],[3,5],[10,11],[3,7],[7,11],[3,14],[2,5],[10,11],[10,12],[2,11],[5,10],[3,5],[10,12],[0,12],[4,5],[8,11],[10,15],[2,11],[2,4],[0,11],[9,13],[2,10],[12,15],[10,11],[2,8],[12,14],[8,13],[1,12],[0,12],[7,9],[2,5],[9,10],[8,13],[12,13],[9,14],[1,6],[6,15],[14,15],[0,1],[7,10],[9,15],[12,14],[3,15],[0,8],[2,15],[0,3],[12,15],[0,1],[9,13],[4,12],[1,6],[7,10],[1,13],[9,11],[7,13],[0,14],[2,14],[12,13],[1,14],[8,13],[1,13],[9,12],[0,11],[8,13],[6,14],[3,5],[6,12],[0,7],[4,7],[0,14],[6,9],[2,14],[14,15],[9,13],[2,13],[4,8],[5,6],[6,14],[4,14],[2,5],[5,8],[3,5],[0,1],[1,13],[0,1],[7,10],[5,14],[0,12],[8,10],[8,14],[6,15],[0,4],[1,2],[1,9],[1,9],[1,11],[2,10],[9,14],[4,12],[7,9],[10,15],[4,15],[4,14],[3,7],[6,10],[7,9],[6,13],[1,11],[0,2],[3,15],[8,15],[4,8],[0,12],[11,12],[7,13],[8,9],[1,5],[2,13],[2,14],[0,14],[1,13],[6,13],[5,7],[8,9],[3,12],[2,10],[2,11],[1,12],[2,7],[1,7],[1,11],[7,13],[11,14],[0,14],[6,10],[0,8],[2,10],[3,5],[3,4],[6,8],[11,14],[0,6],[0,9],[0,4],[3,14],[4,10],[4,13],[3,8],[1,8],[11,14],[2,3],[0,3],[5,6],[5,15],[3,12],[12,14],[3,12],[3,7],[10,15],[2,10],[4,7],[9,15],[13,14],[4,15],[3,14],[0,1],[7,11],[12,15],[1,14],[5,12],[8,11],[6,12],[1,11],[2,4],[0,3],[6,13],[9,12],[3,15],[5,15],[10,13],[3,14],[9,13],[13,14],[4,7]]]
def setup_inputs(rng):
    rt = (0.75 * rng.standard_normal((128, 1), dtype=np.float32) + rng.standard_normal((128, N), dtype=np.float32) / 2).astype(ml_dtypes.bfloat16)
    rm = np.zeros((N, N, TOK), np.float32)
    for r in range(N):
        for t in range(TOK): rm[r, ROUTE[r][t], t] = 1.0
    return {"x": rng.standard_normal((N, 128, TOK), dtype=np.float32).astype(ml_dtypes.bfloat16), "rt": np.broadcast_to(rt, (N, 128, N)).copy(), "rm": rm.astype(ml_dtypes.bfloat16), "w": rng.standard_normal((N, 128, 128), dtype=np.float32).astype(ml_dtypes.bfloat16)}
def setup_inputs_big(rng):
    d = setup_inputs(rng)
    for k in ("x", "w"): d[k] = (d[k].astype(np.float32) * 1024.0).astype(d[k].dtype)
    return d
def setup_inputs_small(rng):
    d = setup_inputs(rng)
    for k in ("x", "w"): d[k] = (d[k].astype(np.float32) * (1 / 1024.0)).astype(d[k].dtype)
    return d
def setup_inputs_apart(rng):
    d = setup_inputs(rng)
    f = (10.0 ** rng.permutation(np.linspace(-1.5, 1.5, N))).astype(np.float32).reshape(N, 1, 1)
    for k in ("x",): d[k] = (d[k].astype(np.float32) * f).astype(d[k].dtype)
    return d
def setup_inputs_lure(rng):
    d = setup_inputs(rng); x = d["x"].astype(np.float32) * 1024; rt = d["rt"][0].astype(np.float32)
    for r in range(N):
        for t in range(TOK):
            u = int(rng.choice([e for e in range(N) if e not in ROUTE[r][t]]))
            x[r][:, t] += 2097152 * (rt[:, u] - rt[:, ROUTE[r][t][0]])
    d["x"] = x.astype(d["x"].dtype)
    return d
def reference(x, rt, rm, w):
    X, RT, W = x.astype(np.float64), rt.astype(np.float64), w.astype(np.float64)
    y = np.zeros((N, 128, TOK))
    for r in range(N):
        sc = RT[r].T @ X[r]
        for t in range(TOK):
            ex = ROUTE[r][t]; g = np.exp(sc[ex, t] - sc[ex, t].max()); g = g / g.sum()
            y[r][:, t] = sum(g[i] * (W[e].T @ X[r][:, t]) for i, e in enumerate(ex))
    return {"y": y.astype(ml_dtypes.bfloat16)}

@@ -1,0 +1,202 @@
+from concourse.bass import DstId, RemoteDMATransfer
+from concourse.mybir import AluOpType, AxisListType, ActivationFunctionType
+
+NR = 16
+TK = 512
+NCH = 4
+NB = 3
+HALF = TK // 2
+
+SCRATCH = {
+    "wd": ("dram", [128, 128], "bfloat16"),
+    "wall": ("sbuf", [128, NR * 128], "bfloat16"),
+    "xs": ("sbuf", [128, TK], "bfloat16"),
+    "rts": ("sbuf", [128, NR], "bfloat16"),
+    "rms": ("sbuf", [NR, TK], "bfloat16"),
+    "ones": ("sbuf", [128, 128], "bfloat16"),
+    "ident": ("sbuf", [128, 128], "bfloat16"),
+    "sel": ("sbuf", [NR, NR * 128], "bfloat16"),
+    "rmT": ("sbuf", [128, NCH * NR], "float32"),
+    "ms": ("sbuf", [128, NCH * NR], "float32"),
+    "nsum": ("sbuf", [128, NCH], "float32"),
+    "sig": ("sbuf", [128, NCH * NR], "float32"),
+    "gT": ("sbuf", [128, NCH * NR], "bfloat16"),
+    "gs": ("sbuf", [NR, TK], "bfloat16"),
+    "xg": ("sbuf", [128, NR * TK], "bfloat16"),
+    "ysb": ("sbuf", [128, TK], "bfloat16"),
+    "p_st": ("psum", [128, 512], "float32"),
+    "p_rm": ("psum", [128, 512], "float32"),
+    "p_gt": ("psum", [128, 512], "float32"),
+    "p_b0": ("psum", [128, 512], "float32"),
+    "p_b1": ("psum", [128, 512], "float32"),
+    "p_b2": ("psum", [128, 512], "float32"),
+    "p_y0": ("psum", [128, 512], "float32"),
+    "p_y1": ("psum", [128, 512], "float32"),
+}
+SEMAPHORES = ["wdl", "xl", "rml", "wown", "hw", "loc", "one", "idn", "sl", "rmt", "st", "v1", "v2", "ns", "sg", "gt",
+              "gtp", "gsl", "bc", "xgs", "y0", "y1", "out", "done"] + ["wa%d" % d for d in range(1, NR)]
+
+
+def _bits(mask):
+    return bin(mask).count("1")
+
+
+def _chip_cores(topo, core):
+    near = range(max(0, core - 16), core + 17)
+    return [c for c in near if c != core and topo.host(c) == topo.host(core) and topo.chip(c) == topo.chip(core)]
+
+
+def _helpers(topo, rank_core):
+    oth = _chip_cores(topo, rank_core)
+    same = [c for c in oth if topo.die(c) == topo.die(rank_core)]
+    far = [c for c in oth if topo.die(c) != topo.die(rank_core)]
+    out = []
+    for i in range(max(len(same), len(far))):
+        if i < len(far):
+            out.append(far[i])
+        if i < len(same):
+            out.append(same[i])
+    return out
+
+
+def _plan(topo, rank_core):
+    hs = _helpers(topo, rank_core)
+    plan = [(rank_core, [1])]
+    for h, c in enumerate(hs):
+        plan.append((c, [d for d in (2 + h, 2 + len(hs) + h) if d < NR]))
+    return plan
+
+
+def _split(mask, parts):
+    bits = [b for b in range(16) if (mask >> b) & 1]
+    per = len(bits) // parts
+    return [sum(1 << b for b in bits[i * per:(i + 1) * per]) for i in range(parts)]
+
+
+def _landing(topo, T, rank, d):
+    src_rank = T.cores[(rank - d) % NR]
+    for c, dists in _plan(topo, src_rank):
+        if d in dists:
+            return _bits(_split(topo.mask(c, T.cores[rank]), len(dists))[dists.index(d)])
+    return 0
+
+
+def _send_w(g, core, T, topo, rank, dists):
+    dst = [T.cores[(rank + d) % NR] for d in dists]
+    masks = _split(topo.mask(core, dst[0]), len(dists))
+    trs = []
+    for d, c, m in zip(dists, dst, masks):
+        rid, pid = topo.addr(c, core)
+        trs.append(RemoteDMATransfer(dst_ids=[DstId(rid=rid, pnc=pid)], dma_engine_mask=m,
+                                     remote_sem=T.sem["wa%d" % d], src=T.wd[:],
+                                     dst=T.wall[:, d * 128:(d + 1) * 128]))
+    g.remote_dma_fused(trs, local_sem=T.sem.loc)
+    return sum(_bits(m) for m in masks)
+
+
+def rank_program(g, core, T, topo):
+    rank = T.rank_of(core)
+    S = T.sem
+    if rank is None:
+        home = [c for c in T.cores if topo.host(c) == topo.host(core) and topo.chip(c) == topo.chip(core)]
+        if not home:
+            return
+        rc = home[0]
+        dists = [ds for c, ds in _plan(topo, rc) if c == core][0]
+        g.wait_ge(S.hw, _bits(topo.mask(rc, core)))
+        n = _send_w(g, core, T, topo, T.rank_of(rc), dists)
+        g.wait_ge(S.loc, n)
+        return
+
+    mult, add = AluOpType.mult, AluOpType.add
+    te, ve, ac, sy = g.tensor, g.vector, g.scalar, g.sync
+    helpers = _helpers(topo, core)
+
+    sy.dma_start(T.wd[:], T.w[:]).then_inc(S.wdl, 16)
+    ac.dma_start(T.xs[:], T.x[:]).then_inc(S.xl, 16)
+    sy.dma_start(T.rms[:], T.rm[:]).then_inc(S.rml, 16)
+    ac.dma_start(T.rts[:], T.rt[:]).then_inc(S.xl, 16)
+    sy.dma_start(T.wall[:, 0:128], T.w[:]).then_inc(S.wown, 16)
+
+    ve.memset(T.ones[:], 1.0).then_inc(S.one, 1)
+    g.wait_ge(S.one, 1)
+    g.affine_select(T.ident[:], T.ones[:], [[-1, 128]], AluOpType.is_equal, 0.0, 0, 1).then_inc(S.idn, 1)
+
+    g.wait_ge(S.wdl, 16)
+    hm = topo.mask(core, helpers[0])
+    ids = []
+    for c in helpers:
+        rid, pid = topo.addr(c, core)
+        ids.append(DstId(rid=rid, pnc=pid))
+    g.remote_dma_fused([RemoteDMATransfer(dst_ids=ids, dma_engine_mask=hm, remote_sem=S.hw, srcs=[T.wd[:]],
+                                          dsts=[T.wd[:] for _ in helpers])], local_sem=S.loc)
+    nloc = _bits(hm) + _send_w(g, core, T, topo, rank, [1])
+    g.wait_ge(S.loc, nloc)
+
+    ve.wait_ge(S.one, 1)
+    ve.wait_ge(S.idn, 1)
+    for e in range(NR):
+        ve.tensor_scalar(T.sel[:, e * 128:(e + 1) * 128], T.ones[0:NR, :], T.ident[0:NR, e:e + 1], None,
+                         mult).then_inc(S.sl, 1)
+
+    te.wait_ge(S.rml, 16)
+    te.wait_ge(S.idn, 1)
+    for c in range(NCH):
+        te.matmul(T.p_rm[:, c * NR:(c + 1) * NR], T.rms[:, c * 128:(c + 1) * 128], T.ident[0:NR, 0:NR], True,
+                  True).then_inc(S.rmt, 1)
+    te.wait_ge(S.xl, 32)
+    for c in range(NCH):
+        te.matmul(T.p_st[:, c * NR:(c + 1) * NR], T.xs[:, c * 128:(c + 1) * 128], T.rts[:], True,
+                  True).then_inc(S.st, 1)
+    W = NCH * NR
+    ve.wait_ge(S.rmt, NCH)
+    ve.tensor_copy(T.rmT[:], T.p_rm[:, 0:W]).then_inc(S.v1, 1)
+    ve.wait_ge(S.st, NCH)
+    ve.wait_ge(S.v1, 1)
+    ve.tensor_tensor(T.ms[:], T.p_st[:, 0:W], T.rmT[:], mult).then_inc(S.v2, 1)
+    ve.wait_ge(S.v2, 1)
+    for c in range(NCH):
+        ve.tensor_reduce(T.nsum[:, c:c + 1], T.ms[:, c * NR:(c + 1) * NR], AxisListType.X, add,
+                         negate=True).then_inc(S.ns, 1)
+    ac.wait_ge(S.ns, NCH)
+    for c in range(NCH):
+        ac.activation(T.sig[:, c * NR:(c + 1) * NR], T.p_st[:, c * NR:(c + 1) * NR], ActivationFunctionType.Sigmoid,
+                      bias=T.nsum[:, c:c + 1], scale=2.0).then_inc(S.sg, 1)
+    ve.wait_ge(S.sg, NCH)
+    ve.tensor_tensor(T.gT[:], T.sig[:], T.rmT[:], mult).then_inc(S.gt, 1)
+    te.wait_ge(S.gt, 1)
+    for c in range(NCH):
+        te.matmul(T.p_gt[0:NR, c * 128:(c + 1) * 128], T.gT[:, c * NR:(c + 1) * NR], T.ident[:], True,
+                  True).then_inc(S.gtp, 1)
+    ve.wait_ge(S.gtp, NCH)
+    ve.tensor_copy(T.gs[:], T.p_gt[0:NR, :]).then_inc(S.gsl, 1)
+
+    pb = [T.p_b0, T.p_b1, T.p_b2]
+    te.wait_ge(S.gsl, 1)
+    te.wait_ge(S.sl, NR)
+    ve.wait_ge(S.xl, 32)
+    for d in range(NR):
+        e = (rank - d) % NR
+        if d >= NB:
+            te.wait_ge(S.xgs, d - NB + 1)
+        te.matmul(pb[d % NB][:], T.sel[:, e * 128:(e + 1) * 128], T.gs[:], True, True).then_inc(S.bc, 1)
+        ve.wait_ge(S.bc, d + 1)
+        ve.tensor_tensor(T.xg[:, d * TK:(d + 1) * TK], T.xs[:], pb[d % NB][:], mult).then_inc(S.xgs, 1)
+
+    for d in range(NR):
+        te.wait_ge(S.xgs, d + 1)
+        if d == 0:
+            te.wait_ge(S.wown, 16)
+        else:
+            te.wait_ge(S["wa%d" % d], _landing(topo, T, rank, d))
+        w_d = T.wall[:, d * 128:(d + 1) * 128]
+        te.matmul(T.p_y0[:, 0:HALF], w_d, T.xg[:, d * TK:d * TK + HALF], d == 0, d == NR - 1).then_inc(S.y0, 1)
+        te.matmul(T.p_y1[:, 0:HALF], w_d, T.xg[:, d * TK + HALF:(d + 1) * TK], d == 0, d == NR - 1).then_inc(S.y1, 1)
+
+    ve.wait_ge(S.y0, NR)
+    ve.tensor_copy(T.ysb[:, 0:HALF], T.p_y0[:, 0:HALF]).then_inc(S.out, 1)
+    ac.wait_ge(S.y1, NR)
+    ac.activation(T.ysb[:, HALF:TK], T.p_y1[:, 0:HALF], ActivationFunctionType.Copy).then_inc(S.out, 1)
+    sy.wait_ge(S.out, 2)
+    sy.dma_start(T.y[:], T.ysb[:]).then_inc(S.done, 16)
+    sy.wait_ge(S.done, 16)

@@ -6,57 +6,66 @@ TK = 512
 NCH = 4
 NB = 3
 HALF = TK // 2
+WORK = [4, 2, 2, 2, 2, 2, 2, 0]
+NMAX = max(WORK)
+NPART = sum(1 for n in WORK[1:] if n)
 
 SCRATCH = {
     "wd": ("dram", [128, 128], "bfloat16"),
-    "wall": ("sbuf", [128, NR * 128], "bfloat16"),
+    "wall": ("sbuf", [128, NMAX * 128], "bfloat16"),
     "xs": ("sbuf", [128, TK], "bfloat16"),
     "rts": ("sbuf", [128, NR], "bfloat16"),
     "rms": ("sbuf", [NR, TK], "bfloat16"),
     "ones": ("sbuf", [128, 128], "bfloat16"),
     "ident": ("sbuf", [128, 128], "bfloat16"),
-    "sel": ("sbuf", [NR, NR * 128], "bfloat16"),
     "rmT": ("sbuf", [128, NCH * NR], "float32"),
     "ms": ("sbuf", [128, NCH * NR], "float32"),
     "nsum": ("sbuf", [128, NCH], "float32"),
     "sig": ("sbuf", [128, NCH * NR], "float32"),
     "gT": ("sbuf", [128, NCH * NR], "bfloat16"),
-    "gs": ("sbuf", [NR, TK], "bfloat16"),
-    "xg": ("sbuf", [128, NR * TK], "bfloat16"),
+    "rep": ("sbuf", [128, NMAX * TK], "bfloat16"),
+    "xg": ("sbuf", [128, NMAX * TK], "bfloat16"),
     "ysb": ("sbuf", [128, TK], "bfloat16"),
+    "part": ("sbuf", [128, NPART * TK], "bfloat16"),
     "p_st": ("psum", [128, 512], "float32"),
     "p_rm": ("psum", [128, 512], "float32"),
-    "p_gt": ("psum", [128, 512], "float32"),
     "p_b0": ("psum", [128, 512], "float32"),
     "p_b1": ("psum", [128, 512], "float32"),
     "p_b2": ("psum", [128, 512], "float32"),
     "p_y0": ("psum", [128, 512], "float32"),
     "p_y1": ("psum", [128, 512], "float32"),
 }
-SEMAPHORES = ["wdl", "xl", "rml", "wown", "hw", "loc", "one", "idn", "sl", "rmt", "st", "v1", "v2", "ns", "sg", "gt",
-              "gtp", "gsl", "bc", "xgs", "y0", "y1", "out", "done"] + ["wa%d" % d for d in range(1, NR)]
+SEMAPHORES = (["wdl", "xl", "rml", "wown", "hw", "xa", "ga", "loc", "one", "idn", "rmt", "st", "v1", "v2", "ns", "sg",
+               "gt", "rb", "bc", "xgs", "y0", "y1", "ad", "out", "done"]
+              + ["wa%d" % i for i in range(NMAX)] + ["pa%d" % j for j in range(NPART)])
 
 
 def _bits(mask):
     return bin(mask).count("1")
 
 
-def _chip_cores(topo, core):
-    near = range(max(0, core - 16), core + 17)
-    return [c for c in near if c != core and topo.host(c) == topo.host(core) and topo.chip(c) == topo.chip(core)]
-
-
 def _helpers(topo, rank_core):
-    oth = _chip_cores(topo, rank_core)
+    near = range(max(0, rank_core - 16), rank_core + 17)
+    oth = [c for c in near if c != rank_core and topo.host(c) == topo.host(rank_core)
+           and topo.chip(c) == topo.chip(rank_core)]
     same = [c for c in oth if topo.die(c) == topo.die(rank_core)]
     far = [c for c in oth if topo.die(c) != topo.die(rank_core)]
     out = []
     for i in range(max(len(same), len(far))):
-        if i < len(far):
-            out.append(far[i])
         if i < len(same):
             out.append(same[i])
+        if i < len(far):
+            out.append(far[i])
     return out
+
+
+def _owner(topo, rank_core):
+    own, d = {}, 0
+    for c, n in zip([rank_core] + _helpers(topo, rank_core), WORK):
+        for i in range(n):
+            own[d] = (c, i)
+            d += 1
+    return own
 
 
 def _plan(topo, rank_core):
@@ -73,44 +82,120 @@ def _split(mask, parts):
     return [sum(1 << b for b in bits[i * per:(i + 1) * per]) for i in range(parts)]
 
 
-def _landing(topo, T, rank, d):
-    src_rank = T.cores[(rank - d) % NR]
-    for c, dists in _plan(topo, src_rank):
+def _landing(topo, T, rank, d, me):
+    for c, dists in _plan(topo, T.cores[(rank - d) % NR]):
         if d in dists:
-            return _bits(_split(topo.mask(c, T.cores[rank]), len(dists))[dists.index(d)])
+            return _bits(_split(topo.mask(c, me), len(dists))[dists.index(d)])
     return 0
 
 
+def _far_mask(topo, T, rc):
+    return topo.mask(rc, T.cores[(T.rank_of(rc) + 1) % NR])
+
+
 def _send_w(g, core, T, topo, rank, dists):
-    dst = [T.cores[(rank + d) % NR] for d in dists]
-    masks = _split(topo.mask(core, dst[0]), len(dists))
+    dst = [_owner(topo, T.cores[(rank + d) % NR])[d] for d in dists]
+    masks = _split(topo.mask(core, dst[0][0]), len(dists))
     trs = []
-    for d, c, m in zip(dists, dst, masks):
+    for (c, i), m in zip(dst, masks):
         rid, pid = topo.addr(c, core)
         trs.append(RemoteDMATransfer(dst_ids=[DstId(rid=rid, pnc=pid)], dma_engine_mask=m,
-                                     remote_sem=T.sem["wa%d" % d], src=T.wd[:],
-                                     dst=T.wall[:, d * 128:(d + 1) * 128]))
+                                     remote_sem=T.sem["wa%d" % i], src=T.wd[:],
+                                     dst=T.wall[:, i * 128:(i + 1) * 128]))
     g.remote_dma_fused(trs, local_sem=T.sem.loc)
     return sum(_bits(m) for m in masks)
+
+
+def _to_all(g, core, T, topo, cores, mask, buf, sem):
+    ids = []
+    for c in cores:
+        rid, pid = topo.addr(c, core)
+        ids.append(DstId(rid=rid, pnc=pid))
+    g.remote_dma_fused([RemoteDMATransfer(dst_ids=ids, dma_engine_mask=mask, remote_sem=sem, srcs=[buf[:]],
+                                          dsts=[buf[:] for _ in cores])], local_sem=T.sem.loc)
+    return _bits(mask)
+
+
+def _experts(g, core, T, topo, rank, ds, more):
+    S, te, ve = T.sem, g.tensor, g.vector
+    pb = [T.p_b0, T.p_b1, T.p_b2]
+    n = len(ds)
+
+    def rep(i):
+        e = (rank - ds[i]) % NR
+        for c in range(NCH):
+            ve.tensor_scalar(T.rep[:, i * TK + c * 128:i * TK + (c + 1) * 128], T.ones[:],
+                             T.gT[:, c * NR + e:c * NR + e + 1], None, AluOpType.mult).then_inc(S.rb, 1)
+
+    rep(0)
+    if n > 1:
+        rep(1)
+    for i in range(n):
+        te.wait_ge(S.rb, NCH * (i + 1))
+        if i >= NB:
+            te.wait_ge(S.xgs, i - NB + 1)
+        for c in range(NCH):
+            te.matmul(pb[i % NB][:, c * 128:(c + 1) * 128], T.rep[:, i * TK + c * 128:i * TK + (c + 1) * 128],
+                      T.ident[:], True, True).then_inc(S.bc, 1)
+        ve.wait_ge(S.bc, NCH * (i + 1))
+        ve.tensor_tensor(T.xg[:, i * TK:(i + 1) * TK], T.xs[:], pb[i % NB][:], AluOpType.mult).then_inc(S.xgs, 1)
+        if i + 2 < n:
+            rep(i + 2)
+    for i, d in enumerate(ds):
+        te.wait_ge(S.xgs, i + 1)
+        if d == 0:
+            te.wait_ge(S.wown, 16)
+        else:
+            te.wait_ge(S["wa%d" % i], _landing(topo, T, rank, d, core))
+        w_i = T.wall[:, i * 128:(i + 1) * 128]
+        te.matmul(T.p_y0[:, 0:HALF], w_i, T.xg[:, i * TK:i * TK + HALF], i == 0,
+                  i == n - 1 and not more).then_inc(S.y0, 1)
+        te.matmul(T.p_y1[:, 0:HALF], w_i, T.xg[:, i * TK + HALF:(i + 1) * TK], i == 0, i == n - 1).then_inc(S.y1, 1)
 
 
 def rank_program(g, core, T, topo):
     rank = T.rank_of(core)
     S = T.sem
+    mult, add = AluOpType.mult, AluOpType.add
+    te, ve, ac, sy = g.tensor, g.vector, g.scalar, g.sync
+    Copy = ActivationFunctionType.Copy
+
     if rank is None:
         home = [c for c in T.cores if topo.host(c) == topo.host(core) and topo.chip(c) == topo.chip(core)]
         if not home:
             return
         rc = home[0]
-        dists = [ds for c, ds in _plan(topo, rc) if c == core][0]
-        g.wait_ge(S.hw, _bits(topo.mask(rc, core)))
-        n = _send_w(g, core, T, topo, T.rank_of(rc), dists)
-        g.wait_ge(S.loc, n)
+        rrank = T.rank_of(rc)
+        ds = [d for d, (c, i) in sorted(_owner(topo, rc).items()) if c == core]
+        if ds:
+            ve.memset(T.ones[:], 1.0).then_inc(S.one, 1)
+            g.wait_ge(S.one, 1)
+            g.affine_select(T.ident[:], T.ones[:], [[-1, 128]], AluOpType.is_equal, 0.0, 0, 1).then_inc(S.idn, 1)
+        g.wait_ge(S.hw, _bits(_far_mask(topo, T, rc)))
+        nloc = _send_w(g, core, T, topo, rrank, [x for c, x in _plan(topo, rc) if c == core][0])
+        if ds:
+            j = [c for c in _helpers(topo, rc) if _owner_has(topo, rc, c)].index(core)
+            full = _bits(topo.mask(rc, core))
+            ve.wait_ge(S.one, 1)
+            ve.wait_ge(S.ga, full)
+            ve.wait_ge(S.xa, full)
+            te.wait_ge(S.idn, 1)
+            _experts(g, core, T, topo, rrank, ds, False)
+            ve.wait_ge(S.y0, len(ds))
+            ve.tensor_copy(T.ysb[:, 0:HALF], T.p_y0[:, 0:HALF]).then_inc(S.out, 1)
+            ac.wait_ge(S.y1, len(ds))
+            ac.activation(T.ysb[:, HALF:TK], T.p_y1[:, 0:HALF], Copy).then_inc(S.out, 1)
+            g.wait_ge(S.out, 2)
+            rid, pid = topo.addr(rc, core)
+            pm = _far_mask(topo, T, rc) & topo.mask(core, rc)
+            g.remote_dma(T.part[:, j * TK:(j + 1) * TK], T.ysb[:], S["pa%d" % j], S.loc, pid, rid, pm)
+            nloc += _bits(pm)
+        g.wait_ge(S.loc, nloc)
         return
 
-    mult, add = AluOpType.mult, AluOpType.add
-    te, ve, ac, sy = g.tensor, g.vector, g.scalar, g.sync
     helpers = _helpers(topo, core)
+    workers = [c for c in helpers if _owner_has(topo, core, c)]
+    ds = [d for d, (c, i) in sorted(_owner(topo, core).items()) if c == core]
 
     sy.dma_start(T.wd[:], T.w[:]).then_inc(S.wdl, 16)
     ac.dma_start(T.xs[:], T.x[:]).then_inc(S.xl, 16)
@@ -123,21 +208,13 @@ def rank_program(g, core, T, topo):
     g.affine_select(T.ident[:], T.ones[:], [[-1, 128]], AluOpType.is_equal, 0.0, 0, 1).then_inc(S.idn, 1)
 
     g.wait_ge(S.wdl, 16)
-    hm = topo.mask(core, helpers[0])
-    ids = []
-    for c in helpers:
-        rid, pid = topo.addr(c, core)
-        ids.append(DstId(rid=rid, pnc=pid))
-    g.remote_dma_fused([RemoteDMATransfer(dst_ids=ids, dma_engine_mask=hm, remote_sem=S.hw, srcs=[T.wd[:]],
-                                          dsts=[T.wd[:] for _ in helpers])], local_sem=S.loc)
-    nloc = _bits(hm) + _send_w(g, core, T, topo, rank, [1])
+    nloc = _to_all(g, core, T, topo, helpers, _far_mask(topo, T, core), T.wd, S.hw)
+    nloc += _send_w(g, core, T, topo, rank, [1])
+    g.wait_ge(S.xl, 32)
+    nloc += _to_all(g, core, T, topo, workers, topo.mask(core, workers[0]), T.xs, S.xa)
+    g.wait_ge(S.gt, 1)
+    nloc += _to_all(g, core, T, topo, workers, topo.mask(core, workers[0]), T.gT, S.ga)
     g.wait_ge(S.loc, nloc)
-
-    ve.wait_ge(S.one, 1)
-    ve.wait_ge(S.idn, 1)
-    for e in range(NR):
-        ve.tensor_scalar(T.sel[:, e * 128:(e + 1) * 128], T.ones[0:NR, :], T.ident[0:NR, e:e + 1], None,
-                         mult).then_inc(S.sl, 1)
 
     te.wait_ge(S.rml, 16)
     te.wait_ge(S.idn, 1)
@@ -164,39 +241,29 @@ def rank_program(g, core, T, topo):
                       bias=T.nsum[:, c:c + 1], scale=2.0).then_inc(S.sg, 1)
     ve.wait_ge(S.sg, NCH)
     ve.tensor_tensor(T.gT[:], T.sig[:], T.rmT[:], mult).then_inc(S.gt, 1)
-    te.wait_ge(S.gt, 1)
-    for c in range(NCH):
-        te.matmul(T.p_gt[0:NR, c * 128:(c + 1) * 128], T.gT[:, c * NR:(c + 1) * NR], T.ident[:], True,
-                  True).then_inc(S.gtp, 1)
-    ve.wait_ge(S.gtp, NCH)
-    ve.tensor_copy(T.gs[:], T.p_gt[0:NR, :]).then_inc(S.gsl, 1)
-
-    pb = [T.p_b0, T.p_b1, T.p_b2]
-    te.wait_ge(S.gsl, 1)
-    te.wait_ge(S.sl, NR)
+    ve.wait_ge(S.gt, 1)
+    ve.wait_ge(S.one, 1)
     ve.wait_ge(S.xl, 32)
-    for d in range(NR):
-        e = (rank - d) % NR
-        if d >= NB:
-            te.wait_ge(S.xgs, d - NB + 1)
-        te.matmul(pb[d % NB][:], T.sel[:, e * 128:(e + 1) * 128], T.gs[:], True, True).then_inc(S.bc, 1)
-        ve.wait_ge(S.bc, d + 1)
-        ve.tensor_tensor(T.xg[:, d * TK:(d + 1) * TK], T.xs[:], pb[d % NB][:], mult).then_inc(S.xgs, 1)
 
-    for d in range(NR):
-        te.wait_ge(S.xgs, d + 1)
-        if d == 0:
-            te.wait_ge(S.wown, 16)
-        else:
-            te.wait_ge(S["wa%d" % d], _landing(topo, T, rank, d))
-        w_d = T.wall[:, d * 128:(d + 1) * 128]
-        te.matmul(T.p_y0[:, 0:HALF], w_d, T.xg[:, d * TK:d * TK + HALF], d == 0, d == NR - 1).then_inc(S.y0, 1)
-        te.matmul(T.p_y1[:, 0:HALF], w_d, T.xg[:, d * TK + HALF:(d + 1) * TK], d == 0, d == NR - 1).then_inc(S.y1, 1)
-
-    ve.wait_ge(S.y0, NR)
-    ve.tensor_copy(T.ysb[:, 0:HALF], T.p_y0[:, 0:HALF]).then_inc(S.out, 1)
-    ac.wait_ge(S.y1, NR)
-    ac.activation(T.ysb[:, HALF:TK], T.p_y1[:, 0:HALF], ActivationFunctionType.Copy).then_inc(S.out, 1)
+    _experts(g, core, T, topo, rank, ds, True)
+    nw = len(workers)
+    ve.wait_ge(S.y1, len(ds))
+    for j, c in enumerate(workers):
+        cnt = _bits(_far_mask(topo, T, core) & topo.mask(c, core))
+        last = j == nw - 1
+        te.wait_ge(S["pa%d" % j], cnt)
+        te.matmul(T.p_y0[:, 0:HALF], T.ident[:], T.part[:, j * TK:j * TK + HALF], False, last).then_inc(S.y0, 1)
+        ve.wait_ge(S["pa%d" % j], cnt)
+        if j:
+            ve.wait_ge(S.ad, j)
+        ve.tensor_tensor(T.ysb[:, HALF:TK] if last else T.p_y1[:, 0:HALF], T.p_y1[:, 0:HALF],
+                         T.part[:, j * TK + HALF:(j + 1) * TK], add).then_inc(S.out if last else S.ad, 1)
+    ac.wait_ge(S.y0, len(ds) + nw)
+    ac.activation(T.ysb[:, 0:HALF], T.p_y0[:, 0:HALF], Copy).then_inc(S.out, 1)
     sy.wait_ge(S.out, 2)
     sy.dma_start(T.y[:], T.ysb[:]).then_inc(S.done, 16)
     sy.wait_ge(S.done, 16)
+
+
+def _owner_has(topo, rank_core, c):
+    return any(w == c for w, i in _owner(topo, rank_core).values())

@@ -6,13 +6,14 @@ TK = 512
 NCH = 4
 NB = 3
 HALF = TK // 2
-WORK = [4, 2, 2, 2, 2, 2, 2, 0]
-NMAX = max(WORK)
-NPART = sum(1 for n in WORK[1:] if n)
+HC = NCH // 2
+NE = 4
+NG = NR // NE
+NPART = 2 * NG - 1
 
 SCRATCH = {
     "wd": ("dram", [128, 128], "bfloat16"),
-    "wall": ("sbuf", [128, NMAX * 128], "bfloat16"),
+    "wall": ("sbuf", [128, NE * 128], "bfloat16"),
     "xs": ("sbuf", [128, TK], "bfloat16"),
     "rts": ("sbuf", [128, NR], "bfloat16"),
     "rms": ("sbuf", [NR, TK], "bfloat16"),
@@ -23,10 +24,10 @@ SCRATCH = {
     "nsum": ("sbuf", [128, NCH], "float32"),
     "sig": ("sbuf", [128, NCH * NR], "float32"),
     "gT": ("sbuf", [128, NCH * NR], "bfloat16"),
-    "rep": ("sbuf", [128, NMAX * TK], "bfloat16"),
-    "xg": ("sbuf", [128, NMAX * TK], "bfloat16"),
+    "rep": ("sbuf", [128, NE * HALF], "bfloat16"),
+    "xg": ("sbuf", [128, NE * HALF], "bfloat16"),
     "ysb": ("sbuf", [128, TK], "bfloat16"),
-    "part": ("sbuf", [128, NPART * TK], "bfloat16"),
+    "part": ("sbuf", [128, NPART * HALF], "bfloat16"),
     "p_st": ("psum", [128, 512], "float32"),
     "p_rm": ("psum", [128, 512], "float32"),
     "p_b0": ("psum", [128, 512], "float32"),
@@ -34,22 +35,27 @@ SCRATCH = {
     "p_b2": ("psum", [128, 512], "float32"),
     "p_y0": ("psum", [128, 512], "float32"),
     "p_y1": ("psum", [128, 512], "float32"),
+    "p_z": ("psum", [128, 512], "float32"),
 }
 SEMAPHORES = (["wdl", "xl", "rml", "wown", "hw", "xa", "ga", "loc", "one", "idn", "rmt", "st", "v1", "v2", "ns", "sg",
-               "gt", "rb", "bc", "xgs", "y0", "y1", "ad", "out", "done"]
-              + ["wa%d" % i for i in range(NMAX)] + ["pa%d" % j for j in range(NPART)])
+               "gt", "rb", "bc", "xgs", "y0", "y1", "ad", "out", "o0", "o1", "dn0", "dn1", "wr"]
+              + ["wa%d" % i for i in range(NE)] + ["pa%d" % j for j in range(NPART)])
 
 
 def _bits(mask):
     return bin(mask).count("1")
 
 
-def _helpers(topo, rank_core):
+def _dies(topo, rank_core):
     near = range(max(0, rank_core - 16), rank_core + 17)
     oth = [c for c in near if c != rank_core and topo.host(c) == topo.host(rank_core)
            and topo.chip(c) == topo.chip(rank_core)]
-    same = [c for c in oth if topo.die(c) == topo.die(rank_core)]
-    far = [c for c in oth if topo.die(c) != topo.die(rank_core)]
+    return ([c for c in oth if topo.die(c) == topo.die(rank_core)],
+            [c for c in oth if topo.die(c) != topo.die(rank_core)])
+
+
+def _helpers(topo, rank_core):
+    same, far = _dies(topo, rank_core)
     out = []
     for i in range(max(len(same), len(far))):
         if i < len(same):
@@ -59,20 +65,23 @@ def _helpers(topo, rank_core):
     return out
 
 
-def _owner(topo, rank_core):
-    own, d = {}, 0
-    for c, n in zip([rank_core] + _helpers(topo, rank_core), WORK):
-        for i in range(n):
-            own[d] = (c, i)
-            d += 1
-    return own
+def _order(topo, rank_core):
+    same, far = _dies(topo, rank_core)
+    return [rank_core] + same + far
+
+
+def _direct(topo, rank_core, d):
+    q, i = d // NE, d % NE
+    s = 1 if q == 0 else (0 if i < NE // 2 else 1)
+    return _order(topo, rank_core)[2 * q + s], i
 
 
 def _plan(topo, rank_core):
     hs = _helpers(topo, rank_core)
-    plan = [(rank_core, [1])]
+    ds = list(range(NE, NR)) + list(range(1, NE))
+    plan = [(rank_core, ds[0:1])]
     for h, c in enumerate(hs):
-        plan.append((c, [d for d in (2 + h, 2 + len(hs) + h) if d < NR]))
+        plan.append((c, ds[1 + 2 * h:3 + 2 * h]))
     return plan
 
 
@@ -89,12 +98,21 @@ def _landing(topo, T, rank, d, me):
     return 0
 
 
+def _turn(topo, T, rank, d):
+    for k, (c, dists) in enumerate(_plan(topo, T.cores[(rank - d) % NR])):
+        if d in dists:
+            return k
+    return 0
+
+
 def _far_mask(topo, T, rc):
     return topo.mask(rc, T.cores[(T.rank_of(rc) + 1) % NR])
 
 
-def _send_w(g, core, T, topo, rank, dists):
-    dst = [_owner(topo, T.cores[(rank + d) % NR])[d] for d in dists]
+def _send_w(g, core, T, topo, rc):
+    rank = T.rank_of(rc)
+    dists = [x for c, x in _plan(topo, rc) if c == core][0]
+    dst = [_direct(topo, T.cores[(rank + d) % NR], d) for d in dists]
     masks = _split(topo.mask(core, dst[0][0]), len(dists))
     trs = []
     for (c, i), m in zip(dst, masks):
@@ -106,51 +124,64 @@ def _send_w(g, core, T, topo, rank, dists):
     return sum(_bits(m) for m in masks)
 
 
-def _to_all(g, core, T, topo, cores, mask, buf, sem):
-    ids = []
+def _ids(topo, core, cores):
+    out = []
     for c in cores:
         rid, pid = topo.addr(c, core)
-        ids.append(DstId(rid=rid, pnc=pid))
-    g.remote_dma_fused([RemoteDMATransfer(dst_ids=ids, dma_engine_mask=mask, remote_sem=sem, srcs=[buf[:]],
-                                          dsts=[buf[:] for _ in cores])], local_sem=T.sem.loc)
+        out.append(DstId(rid=rid, pnc=pid))
+    return out
+
+
+def _to_all(g, core, T, topo, cores, mask, buf, sem):
+    g.remote_dma_fused([RemoteDMATransfer(dst_ids=_ids(topo, core, cores), dma_engine_mask=mask, remote_sem=sem,
+                                          srcs=[buf[:]], dsts=[buf[:] for _ in cores])], local_sem=T.sem.loc)
     return _bits(mask)
 
 
-def _experts(g, core, T, topo, rank, ds, more):
+def _experts(g, core, T, topo, rc, q, s, more):
     S, te, ve = T.sem, g.tensor, g.vector
+    rank = T.rank_of(rc)
     pb = [T.p_b0, T.p_b1, T.p_b2]
-    n = len(ds)
+    n = NE
+    twin = _order(topo, rc)[2 * q + 1 - s]
 
     def rep(i):
-        e = (rank - ds[i]) % NR
-        for c in range(NCH):
-            ve.tensor_scalar(T.rep[:, i * TK + c * 128:i * TK + (c + 1) * 128], T.ones[:],
-                             T.gT[:, c * NR + e:c * NR + e + 1], None, AluOpType.mult).then_inc(S.rb, 1)
+        e = (rank - (NE * q + i)) % NR
+        for c in range(HC):
+            col = (HC * s + c) * NR + e
+            ve.tensor_scalar(T.rep[:, i * HALF + c * 128:i * HALF + (c + 1) * 128], T.ones[:],
+                             T.gT[:, col:col + 1], None, AluOpType.mult).then_inc(S.rb, 1)
 
     rep(0)
-    if n > 1:
-        rep(1)
+    rep(1)
     for i in range(n):
-        te.wait_ge(S.rb, NCH * (i + 1))
+        te.wait_ge(S.rb, HC * (i + 1))
         if i >= NB:
             te.wait_ge(S.xgs, i - NB + 1)
-        for c in range(NCH):
-            te.matmul(pb[i % NB][:, c * 128:(c + 1) * 128], T.rep[:, i * TK + c * 128:i * TK + (c + 1) * 128],
+        for c in range(HC):
+            te.matmul(pb[i % NB][:, c * 128:(c + 1) * 128], T.rep[:, i * HALF + c * 128:i * HALF + (c + 1) * 128],
                       T.ident[:], True, True).then_inc(S.bc, 1)
-        ve.wait_ge(S.bc, NCH * (i + 1))
-        ve.tensor_tensor(T.xg[:, i * TK:(i + 1) * TK], T.xs[:], pb[i % NB][:], AluOpType.mult).then_inc(S.xgs, 1)
+        ve.wait_ge(S.bc, HC * (i + 1))
+        ve.tensor_tensor(T.xg[:, i * HALF:(i + 1) * HALF], T.xs[:, 0:HALF], pb[i % NB][:, 0:HALF],
+                         AluOpType.mult).then_inc(S.xgs, 1)
         if i + 2 < n:
             rep(i + 2)
-    for i, d in enumerate(ds):
-        te.wait_ge(S.xgs, i + 1)
+    kind = {}
+    for i in range(n):
+        d = NE * q + i
         if d == 0:
-            te.wait_ge(S.wown, 16)
+            kind[i] = (0, 0, S.wown, 16)
+        elif _direct(topo, rc, d)[0] == core:
+            kind[i] = (1, _turn(topo, T, rank, d), S["wa%d" % i], _landing(topo, T, rank, d, core))
         else:
-            te.wait_ge(S["wa%d" % i], _landing(topo, T, rank, d, core))
+            kind[i] = (2, i, S.wr, _bits(_far_mask(topo, T, rc) & topo.mask(twin, core)))
+    te.wait_ge(S.xgs, n)
+    for k, i in enumerate(sorted(range(n), key=lambda i: kind[i][0:2])):
+        te.wait_ge(kind[i][2], kind[i][3])
         w_i = T.wall[:, i * 128:(i + 1) * 128]
-        te.matmul(T.p_y0[:, 0:HALF], w_i, T.xg[:, i * TK:i * TK + HALF], i == 0,
-                  i == n - 1 and not more).then_inc(S.y0, 1)
-        te.matmul(T.p_y1[:, 0:HALF], w_i, T.xg[:, i * TK + HALF:(i + 1) * TK], i == 0, i == n - 1).then_inc(S.y1, 1)
+        stop = k == n - 1 and not more
+        te.matmul(T.p_y0[:, 0:128], w_i, T.xg[:, i * HALF:i * HALF + 128], k == 0, stop).then_inc(S.y0, 1)
+        te.matmul(T.p_y1[:, 0:128], w_i, T.xg[:, i * HALF + 128:(i + 1) * HALF], k == 0, stop).then_inc(S.y1, 1)
 
 
 def rank_program(g, core, T, topo):
@@ -166,36 +197,47 @@ def rank_program(g, core, T, topo):
             return
         rc = home[0]
         rrank = T.rank_of(rc)
-        ds = [d for d, (c, i) in sorted(_owner(topo, rc).items()) if c == core]
-        if ds:
-            ve.memset(T.ones[:], 1.0).then_inc(S.one, 1)
-            g.wait_ge(S.one, 1)
-            g.affine_select(T.ident[:], T.ones[:], [[-1, 128]], AluOpType.is_equal, 0.0, 0, 1).then_inc(S.idn, 1)
-        g.wait_ge(S.hw, _bits(_far_mask(topo, T, rc)))
-        nloc = _send_w(g, core, T, topo, rrank, [x for c, x in _plan(topo, rc) if c == core][0])
-        if ds:
-            j = [c for c in _helpers(topo, rc) if _owner_has(topo, rc, c)].index(core)
-            full = _bits(topo.mask(rc, core))
-            ve.wait_ge(S.one, 1)
-            ve.wait_ge(S.ga, full)
-            ve.wait_ge(S.xa, full)
-            te.wait_ge(S.idn, 1)
-            _experts(g, core, T, topo, rrank, ds, False)
-            ve.wait_ge(S.y0, len(ds))
-            ve.tensor_copy(T.ysb[:, 0:HALF], T.p_y0[:, 0:HALF]).then_inc(S.out, 1)
-            ac.wait_ge(S.y1, len(ds))
-            ac.activation(T.ysb[:, HALF:TK], T.p_y1[:, 0:HALF], Copy).then_inc(S.out, 1)
-            g.wait_ge(S.out, 2)
-            rid, pid = topo.addr(rc, core)
-            pm = _far_mask(topo, T, rc) & topo.mask(core, rc)
-            g.remote_dma(T.part[:, j * TK:(j + 1) * TK], T.ysb[:], S["pa%d" % j], S.loc, pid, rid, pm)
-            nloc += _bits(pm)
+        order = _order(topo, rc)
+        j = order.index(core) - 1
+        q, s = (j + 1) // 2, (j + 1) % 2
+        twin = order[2 * q + 1 - s]
+        nfar = _bits(_far_mask(topo, T, rc))
+        ve.memset(T.ones[:], 1.0).then_inc(S.one, 1)
+        g.wait_ge(S.one, 1)
+        g.affine_select(T.ident[:], T.ones[:], [[-1, 128]], AluOpType.is_equal, 0.0, 0, 1).then_inc(S.idn, 1)
+        g.wait_ge(S.hw, nfar)
+        nloc = _send_w(g, core, T, topo, rc)
+        if q == 0:
+            sy.wait_ge(S.hw, nfar)
+            sy.dma_start(T.wall[:, 0:128], T.wd[:]).then_inc(S.wown, 16)
+        mine = [i for i in range(NE) if NE * q + i and _direct(topo, rc, NE * q + i)[0] == core]
+        tm = _far_mask(topo, T, rc) & topo.mask(core, twin)
+        rid, pid = topo.addr(twin, core)
+        for i in mine:
+            g.wait_ge(S["wa%d" % i], _landing(topo, T, rrank, NE * q + i, core))
+        lo, hi = mine[0] * 128, (mine[-1] + 1) * 128
+        g.remote_dma(T.wall[:, lo:hi], T.wall[:, lo:hi], S.wr, S.loc, pid, rid, tm)
+        nloc += _bits(tm)
+        ve.wait_ge(S.one, 1)
+        ve.wait_ge(S.ga, _bits(topo.mask(rc, core)))
+        ve.wait_ge(S.xa, _bits(_split(topo.mask(rc, core), 2)[s]))
+        te.wait_ge(S.idn, 1)
+        _experts(g, core, T, topo, rc, q, s, False)
+        ve.wait_ge(S.y0, NE)
+        ve.tensor_copy(T.ysb[:, 0:128], T.p_y0[:, 0:128]).then_inc(S.out, 1)
+        ac.wait_ge(S.y1, NE)
+        ac.activation(T.ysb[:, 128:HALF], T.p_y1[:, 0:128], Copy).then_inc(S.out, 1)
+        g.wait_ge(S.out, 2)
+        rid, pid = topo.addr(rc, core)
+        pm = _far_mask(topo, T, rc) & topo.mask(core, rc)
+        g.remote_dma(T.part[:, j * HALF:(j + 1) * HALF], T.ysb[:, 0:HALF], S["pa%d" % j], S.loc, pid, rid, pm)
+        nloc += _bits(pm)
         g.wait_ge(S.loc, nloc)
         return
 
     helpers = _helpers(topo, core)
-    workers = [c for c in helpers if _owner_has(topo, core, c)]
-    ds = [d for d, (c, i) in sorted(_owner(topo, core).items()) if c == core]
+    order = _order(topo, core)
+    others = order[1:]
 
     sy.dma_start(T.wd[:], T.w[:]).then_inc(S.wdl, 16)
     ac.dma_start(T.xs[:], T.x[:]).then_inc(S.xl, 16)
@@ -209,11 +251,18 @@ def rank_program(g, core, T, topo):
 
     g.wait_ge(S.wdl, 16)
     nloc = _to_all(g, core, T, topo, helpers, _far_mask(topo, T, core), T.wd, S.hw)
-    nloc += _send_w(g, core, T, topo, rank, [1])
     g.wait_ge(S.xl, 32)
-    nloc += _to_all(g, core, T, topo, workers, topo.mask(core, workers[0]), T.xs, S.xa)
+    xm = _split(topo.mask(core, others[0]), 2)
+    trs = []
+    for s in range(2):
+        cs = [order[2 * q + s] for q in range(NG) if 2 * q + s]
+        trs.append(RemoteDMATransfer(dst_ids=_ids(topo, core, cs), dma_engine_mask=xm[s], remote_sem=S.xa,
+                                     srcs=[T.xs[:, s * HALF:(s + 1) * HALF]], dsts=[T.xs[:, 0:HALF] for _ in cs]))
+        nloc += _bits(xm[s])
+    g.remote_dma_fused(trs, local_sem=S.loc)
+    nloc += _send_w(g, core, T, topo, core)
     g.wait_ge(S.gt, 1)
-    nloc += _to_all(g, core, T, topo, workers, topo.mask(core, workers[0]), T.gT, S.ga)
+    nloc += _to_all(g, core, T, topo, others, topo.mask(core, others[0]), T.gT, S.ga)
     g.wait_ge(S.loc, nloc)
 
     te.wait_ge(S.rml, 16)
@@ -245,25 +294,36 @@ def rank_program(g, core, T, topo):
     ve.wait_ge(S.one, 1)
     ve.wait_ge(S.xl, 32)
 
-    _experts(g, core, T, topo, rank, ds, True)
-    nw = len(workers)
-    ve.wait_ge(S.y1, len(ds))
-    for j, c in enumerate(workers):
-        cnt = _bits(_far_mask(topo, T, core) & topo.mask(c, core))
-        last = j == nw - 1
-        te.wait_ge(S["pa%d" % j], cnt)
-        te.matmul(T.p_y0[:, 0:HALF], T.ident[:], T.part[:, j * TK:j * TK + HALF], False, last).then_inc(S.y0, 1)
-        ve.wait_ge(S["pa%d" % j], cnt)
-        if j:
-            ve.wait_ge(S.ad, j)
-        ve.tensor_tensor(T.ysb[:, HALF:TK] if last else T.p_y1[:, 0:HALF], T.p_y1[:, 0:HALF],
-                         T.part[:, j * TK + HALF:(j + 1) * TK], add).then_inc(S.out if last else S.ad, 1)
-    ac.wait_ge(S.y0, len(ds) + nw)
-    ac.activation(T.ysb[:, 0:HALF], T.p_y0[:, 0:HALF], Copy).then_inc(S.out, 1)
-    sy.wait_ge(S.out, 2)
-    sy.dma_start(T.y[:], T.ysb[:]).then_inc(S.done, 16)
-    sy.wait_ge(S.done, 16)
+    _experts(g, core, T, topo, core, 0, 0, True)
 
+    def cnt(j):
+        return _bits(_far_mask(topo, T, core) & topo.mask(others[j], core))
 
-def _owner_has(topo, rank_core, c):
-    return any(w == c for w, i in _owner(topo, rank_core).values())
+    js = [2 * q - 1 for q in range(1, NG)]
+    for k, j in enumerate(js):
+        last = k == len(js) - 1
+        te.wait_ge(S["pa%d" % j], cnt(j))
+        te.matmul(T.p_y0[:, 0:128], T.ident[:], T.part[:, j * HALF:j * HALF + 128], False, last).then_inc(S.y0, 1)
+        te.matmul(T.p_y1[:, 0:128], T.ident[:], T.part[:, j * HALF + 128:(j + 1) * HALF], False,
+                  last).then_inc(S.y1, 1)
+    ac.wait_ge(S.y0, NE + len(js))
+    ac.activation(T.ysb[:, 0:128], T.p_y0[:, 0:128], Copy).then_inc(S.o0, 1)
+    ac.wait_ge(S.y1, NE + len(js))
+    ac.activation(T.ysb[:, 128:HALF], T.p_y1[:, 0:128], Copy).then_inc(S.o0, 1)
+    ac.wait_ge(S.o0, 2)
+    ac.dma_start(T.y[:, 0:HALF], T.ysb[:, 0:HALF]).then_inc(S.dn0, 16)
+    ac.wait_ge(S.dn0, 16)
+    j1 = [2 * q for q in range(NG)]
+    for k in range(1, len(j1)):
+        if k == 1:
+            ve.wait_ge(S["pa%d" % j1[0]], cnt(j1[0]))
+        else:
+            ve.wait_ge(S.ad, k - 1)
+        ve.wait_ge(S["pa%d" % j1[k]], cnt(j1[k]))
+        last = k == len(j1) - 1
+        ve.tensor_tensor(T.ysb[:, HALF:TK] if last else T.p_z[:, 0:HALF],
+                         T.part[:, j1[0] * HALF:(j1[0] + 1) * HALF] if k == 1 else T.p_z[:, 0:HALF],
+                         T.part[:, j1[k] * HALF:(j1[k] + 1) * HALF], add).then_inc(S.o1 if last else S.ad, 1)
+    sy.wait_ge(S.o1, 1)
+    sy.dma_start(T.y[:, HALF:TK], T.ysb[:, HALF:TK]).then_inc(S.dn1, 16)
+    sy.wait_ge(S.dn1, 16)

from concourse.bass import DstId, RemoteDMATransfer
from concourse.mybir import AluOpType, AxisListType, ActivationFunctionType

NR = 16
TK = 512
NCH = 4
NB = 3
HALF = TK // 2
HC = NCH // 2
NE = 4
NG = NR // NE
NPART = 2 * NG - 1

SCRATCH = {
    "wd": ("dram", [128, 128], "bfloat16"),
    "wall": ("sbuf", [128, NE * 128], "bfloat16"),
    "xs": ("sbuf", [128, TK], "bfloat16"),
    "rts": ("sbuf", [128, NR], "bfloat16"),
    "rms": ("sbuf", [NR, TK], "bfloat16"),
    "ones": ("sbuf", [128, 128], "bfloat16"),
    "ident": ("sbuf", [128, 128], "bfloat16"),
    "rmT": ("sbuf", [128, NCH * NR], "float32"),
    "ms": ("sbuf", [128, NCH * NR], "float32"),
    "nsum": ("sbuf", [128, NCH], "float32"),
    "sig": ("sbuf", [128, NCH * NR], "float32"),
    "gT": ("sbuf", [128, NCH * NR], "bfloat16"),
    "rep": ("sbuf", [128, NE * HALF], "bfloat16"),
    "xg": ("sbuf", [128, NE * HALF], "bfloat16"),
    "ysb": ("sbuf", [128, TK], "bfloat16"),
    "part": ("sbuf", [128, NPART * HALF], "bfloat16"),
    "p_st": ("psum", [128, 512], "float32"),
    "p_rm": ("psum", [128, 512], "float32"),
    "p_b0": ("psum", [128, 512], "float32"),
    "p_b1": ("psum", [128, 512], "float32"),
    "p_b2": ("psum", [128, 512], "float32"),
    "p_y0": ("psum", [128, 512], "float32"),
    "p_y1": ("psum", [128, 512], "float32"),
    "p_z": ("psum", [128, 512], "float32"),
}
SEMAPHORES = (["wdl", "xl", "rml", "wown", "hw", "xa", "ga", "loc", "one", "idn", "rmt", "st", "v1", "v2", "ns", "sg",
               "gt", "rb", "bc", "xgs", "y0", "y1", "ad", "out", "o0", "o1", "dn0", "dn1", "wr"]
              + ["wa%d" % i for i in range(NE)] + ["pa%d" % j for j in range(NPART)])


def _bits(mask):
    return bin(mask).count("1")


def _dies(topo, rank_core):
    near = range(max(0, rank_core - 16), rank_core + 17)
    oth = [c for c in near if c != rank_core and topo.host(c) == topo.host(rank_core)
           and topo.chip(c) == topo.chip(rank_core)]
    return ([c for c in oth if topo.die(c) == topo.die(rank_core)],
            [c for c in oth if topo.die(c) != topo.die(rank_core)])


def _helpers(topo, rank_core):
    same, far = _dies(topo, rank_core)
    out = []
    for i in range(max(len(same), len(far))):
        if i < len(same):
            out.append(same[i])
        if i < len(far):
            out.append(far[i])
    return out


def _order(topo, rank_core):
    same, far = _dies(topo, rank_core)
    return [rank_core] + same + far


def _direct(topo, rank_core, d):
    q, i = d // NE, d % NE
    s = 1 if q == 0 else (0 if i < NE // 2 else 1)
    return _order(topo, rank_core)[2 * q + s], i


def _plan(topo, rank_core):
    hs = _helpers(topo, rank_core)
    ds = list(range(NE, NR)) + list(range(1, NE))
    plan = [(rank_core, ds[0:1])]
    for h, c in enumerate(hs):
        plan.append((c, ds[1 + 2 * h:3 + 2 * h]))
    return plan


def _split(mask, parts):
    bits = [b for b in range(16) if (mask >> b) & 1]
    per = len(bits) // parts
    return [sum(1 << b for b in bits[i * per:(i + 1) * per]) for i in range(parts)]


def _landing(topo, T, rank, d, me):
    for c, dists in _plan(topo, T.cores[(rank - d) % NR]):
        if d in dists:
            return _bits(_split(topo.mask(c, me), len(dists))[dists.index(d)])
    return 0


def _turn(topo, T, rank, d):
    for k, (c, dists) in enumerate(_plan(topo, T.cores[(rank - d) % NR])):
        if d in dists:
            return k
    return 0


def _far_mask(topo, T, rc):
    return topo.mask(rc, T.cores[(T.rank_of(rc) + 1) % NR])


def _send_w(g, core, T, topo, rc):
    rank = T.rank_of(rc)
    dists = [x for c, x in _plan(topo, rc) if c == core][0]
    dst = [_direct(topo, T.cores[(rank + d) % NR], d) for d in dists]
    masks = _split(topo.mask(core, dst[0][0]), len(dists))
    trs = []
    for (c, i), m in zip(dst, masks):
        rid, pid = topo.addr(c, core)
        trs.append(RemoteDMATransfer(dst_ids=[DstId(rid=rid, pnc=pid)], dma_engine_mask=m,
                                     remote_sem=T.sem["wa%d" % i], src=T.wd[:],
                                     dst=T.wall[:, i * 128:(i + 1) * 128]))
    g.remote_dma_fused(trs, local_sem=T.sem.loc)
    return sum(_bits(m) for m in masks)


def _ids(topo, core, cores):
    out = []
    for c in cores:
        rid, pid = topo.addr(c, core)
        out.append(DstId(rid=rid, pnc=pid))
    return out


def _to_all(g, core, T, topo, cores, mask, buf, sem):
    g.remote_dma_fused([RemoteDMATransfer(dst_ids=_ids(topo, core, cores), dma_engine_mask=mask, remote_sem=sem,
                                          srcs=[buf[:]], dsts=[buf[:] for _ in cores])], local_sem=T.sem.loc)
    return _bits(mask)


def _experts(g, core, T, topo, rc, q, s, more):
    S, te, ve = T.sem, g.tensor, g.vector
    rank = T.rank_of(rc)
    pb = [T.p_b0, T.p_b1, T.p_b2]
    n = NE
    twin = _order(topo, rc)[2 * q + 1 - s]

    def rep(i):
        e = (rank - (NE * q + i)) % NR
        for c in range(HC):
            col = (HC * s + c) * NR + e
            ve.tensor_scalar(T.rep[:, i * HALF + c * 128:i * HALF + (c + 1) * 128], T.ones[:],
                             T.gT[:, col:col + 1], None, AluOpType.mult).then_inc(S.rb, 1)

    rep(0)
    rep(1)
    for i in range(n):
        te.wait_ge(S.rb, HC * (i + 1))
        if i >= NB:
            te.wait_ge(S.xgs, i - NB + 1)
        for c in range(HC):
            te.matmul(pb[i % NB][:, c * 128:(c + 1) * 128], T.rep[:, i * HALF + c * 128:i * HALF + (c + 1) * 128],
                      T.ident[:], True, True).then_inc(S.bc, 1)
        ve.wait_ge(S.bc, HC * (i + 1))
        ve.tensor_tensor(T.xg[:, i * HALF:(i + 1) * HALF], T.xs[:, 0:HALF], pb[i % NB][:, 0:HALF],
                         AluOpType.mult).then_inc(S.xgs, 1)
        if i + 2 < n:
            rep(i + 2)
    kind = {}
    for i in range(n):
        d = NE * q + i
        if d == 0:
            kind[i] = (0, 0, S.wown, 16)
        elif _direct(topo, rc, d)[0] == core:
            kind[i] = (1, _turn(topo, T, rank, d), S["wa%d" % i], _landing(topo, T, rank, d, core))
        else:
            kind[i] = (2, i, S.wr, _bits(_far_mask(topo, T, rc) & topo.mask(twin, core)))
    te.wait_ge(S.xgs, n)
    for k, i in enumerate(sorted(range(n), key=lambda i: kind[i][0:2])):
        te.wait_ge(kind[i][2], kind[i][3])
        w_i = T.wall[:, i * 128:(i + 1) * 128]
        stop = k == n - 1 and not more
        te.matmul(T.p_y0[:, 0:128], w_i, T.xg[:, i * HALF:i * HALF + 128], k == 0, stop).then_inc(S.y0, 1)
        te.matmul(T.p_y1[:, 0:128], w_i, T.xg[:, i * HALF + 128:(i + 1) * HALF], k == 0, stop).then_inc(S.y1, 1)


def rank_program(g, core, T, topo):
    rank = T.rank_of(core)
    S = T.sem
    mult, add = AluOpType.mult, AluOpType.add
    te, ve, ac, sy = g.tensor, g.vector, g.scalar, g.sync
    Copy = ActivationFunctionType.Copy

    if rank is None:
        home = [c for c in T.cores if topo.host(c) == topo.host(core) and topo.chip(c) == topo.chip(core)]
        if not home:
            return
        rc = home[0]
        rrank = T.rank_of(rc)
        order = _order(topo, rc)
        j = order.index(core) - 1
        q, s = (j + 1) // 2, (j + 1) % 2
        twin = order[2 * q + 1 - s]
        nfar = _bits(_far_mask(topo, T, rc))
        ve.memset(T.ones[:], 1.0).then_inc(S.one, 1)
        g.wait_ge(S.one, 1)
        g.affine_select(T.ident[:], T.ones[:], [[-1, 128]], AluOpType.is_equal, 0.0, 0, 1).then_inc(S.idn, 1)
        g.wait_ge(S.hw, nfar)
        nloc = _send_w(g, core, T, topo, rc)
        if q == 0:
            sy.wait_ge(S.hw, nfar)
            sy.dma_start(T.wall[:, 0:128], T.wd[:]).then_inc(S.wown, 16)
        mine = [i for i in range(NE) if NE * q + i and _direct(topo, rc, NE * q + i)[0] == core]
        tm = _far_mask(topo, T, rc) & topo.mask(core, twin)
        rid, pid = topo.addr(twin, core)
        for i in mine:
            g.wait_ge(S["wa%d" % i], _landing(topo, T, rrank, NE * q + i, core))
        lo, hi = mine[0] * 128, (mine[-1] + 1) * 128
        g.remote_dma(T.wall[:, lo:hi], T.wall[:, lo:hi], S.wr, S.loc, pid, rid, tm)
        nloc += _bits(tm)
        ve.wait_ge(S.one, 1)
        ve.wait_ge(S.ga, _bits(topo.mask(rc, core)))
        ve.wait_ge(S.xa, _bits(_split(topo.mask(rc, core), 2)[s]))
        te.wait_ge(S.idn, 1)
        _experts(g, core, T, topo, rc, q, s, False)
        ve.wait_ge(S.y0, NE)
        ve.tensor_copy(T.ysb[:, 0:128], T.p_y0[:, 0:128]).then_inc(S.out, 1)
        ac.wait_ge(S.y1, NE)
        ac.activation(T.ysb[:, 128:HALF], T.p_y1[:, 0:128], Copy).then_inc(S.out, 1)
        g.wait_ge(S.out, 2)
        rid, pid = topo.addr(rc, core)
        pm = _far_mask(topo, T, rc) & topo.mask(core, rc)
        g.remote_dma(T.part[:, j * HALF:(j + 1) * HALF], T.ysb[:, 0:HALF], S["pa%d" % j], S.loc, pid, rid, pm)
        nloc += _bits(pm)
        g.wait_ge(S.loc, nloc)
        return

    helpers = _helpers(topo, core)
    order = _order(topo, core)
    others = order[1:]

    sy.dma_start(T.wd[:], T.w[:]).then_inc(S.wdl, 16)
    ac.dma_start(T.xs[:], T.x[:]).then_inc(S.xl, 16)
    sy.dma_start(T.rms[:], T.rm[:]).then_inc(S.rml, 16)
    ac.dma_start(T.rts[:], T.rt[:]).then_inc(S.xl, 16)
    sy.dma_start(T.wall[:, 0:128], T.w[:]).then_inc(S.wown, 16)

    ve.memset(T.ones[:], 1.0).then_inc(S.one, 1)
    g.wait_ge(S.one, 1)
    g.affine_select(T.ident[:], T.ones[:], [[-1, 128]], AluOpType.is_equal, 0.0, 0, 1).then_inc(S.idn, 1)

    g.wait_ge(S.wdl, 16)
    nloc = _to_all(g, core, T, topo, helpers, _far_mask(topo, T, core), T.wd, S.hw)
    g.wait_ge(S.xl, 32)
    xm = _split(topo.mask(core, others[0]), 2)
    trs = []
    for s in range(2):
        cs = [order[2 * q + s] for q in range(NG) if 2 * q + s]
        trs.append(RemoteDMATransfer(dst_ids=_ids(topo, core, cs), dma_engine_mask=xm[s], remote_sem=S.xa,
                                     srcs=[T.xs[:, s * HALF:(s + 1) * HALF]], dsts=[T.xs[:, 0:HALF] for _ in cs]))
        nloc += _bits(xm[s])
    g.remote_dma_fused(trs, local_sem=S.loc)
    nloc += _send_w(g, core, T, topo, core)
    g.wait_ge(S.gt, 1)
    nloc += _to_all(g, core, T, topo, others, topo.mask(core, others[0]), T.gT, S.ga)
    g.wait_ge(S.loc, nloc)

    te.wait_ge(S.rml, 16)
    te.wait_ge(S.idn, 1)
    for c in range(NCH):
        te.matmul(T.p_rm[:, c * NR:(c + 1) * NR], T.rms[:, c * 128:(c + 1) * 128], T.ident[0:NR, 0:NR], True,
                  True).then_inc(S.rmt, 1)
    te.wait_ge(S.xl, 32)
    for c in range(NCH):
        te.matmul(T.p_st[:, c * NR:(c + 1) * NR], T.xs[:, c * 128:(c + 1) * 128], T.rts[:], True,
                  True).then_inc(S.st, 1)
    W = NCH * NR
    ve.wait_ge(S.rmt, NCH)
    ve.tensor_copy(T.rmT[:], T.p_rm[:, 0:W]).then_inc(S.v1, 1)
    ve.wait_ge(S.st, NCH)
    ve.wait_ge(S.v1, 1)
    ve.tensor_tensor(T.ms[:], T.p_st[:, 0:W], T.rmT[:], mult).then_inc(S.v2, 1)
    ve.wait_ge(S.v2, 1)
    for c in range(NCH):
        ve.tensor_reduce(T.nsum[:, c:c + 1], T.ms[:, c * NR:(c + 1) * NR], AxisListType.X, add,
                         negate=True).then_inc(S.ns, 1)
    ac.wait_ge(S.ns, NCH)
    for c in range(NCH):
        ac.activation(T.sig[:, c * NR:(c + 1) * NR], T.p_st[:, c * NR:(c + 1) * NR], ActivationFunctionType.Sigmoid,
                      bias=T.nsum[:, c:c + 1], scale=2.0).then_inc(S.sg, 1)
    ve.wait_ge(S.sg, NCH)
    ve.tensor_tensor(T.gT[:], T.sig[:], T.rmT[:], mult).then_inc(S.gt, 1)
    ve.wait_ge(S.gt, 1)
    ve.wait_ge(S.one, 1)
    ve.wait_ge(S.xl, 32)

    _experts(g, core, T, topo, core, 0, 0, True)

    def cnt(j):
        return _bits(_far_mask(topo, T, core) & topo.mask(others[j], core))

    js = [2 * q - 1 for q in range(1, NG)]
    for k, j in enumerate(js):
        last = k == len(js) - 1
        te.wait_ge(S["pa%d" % j], cnt(j))
        te.matmul(T.p_y0[:, 0:128], T.ident[:], T.part[:, j * HALF:j * HALF + 128], False, last).then_inc(S.y0, 1)
        te.matmul(T.p_y1[:, 0:128], T.ident[:], T.part[:, j * HALF + 128:(j + 1) * HALF], False,
                  last).then_inc(S.y1, 1)
    ac.wait_ge(S.y0, NE + len(js))
    ac.activation(T.ysb[:, 0:128], T.p_y0[:, 0:128], Copy).then_inc(S.o0, 1)
    ac.wait_ge(S.y1, NE + len(js))
    ac.activation(T.ysb[:, 128:HALF], T.p_y1[:, 0:128], Copy).then_inc(S.o0, 1)
    ac.wait_ge(S.o0, 2)
    ac.dma_start(T.y[:, 0:HALF], T.ysb[:, 0:HALF]).then_inc(S.dn0, 16)
    ac.wait_ge(S.dn0, 16)
    j1 = [2 * q for q in range(NG)]
    for k in range(1, len(j1)):
        if k == 1:
            ve.wait_ge(S["pa%d" % j1[0]], cnt(j1[0]))
        else:
            ve.wait_ge(S.ad, k - 1)
        ve.wait_ge(S["pa%d" % j1[k]], cnt(j1[k]))
        last = k == len(j1) - 1
        ve.tensor_tensor(T.ysb[:, HALF:TK] if last else T.p_z[:, 0:HALF],
                         T.part[:, j1[0] * HALF:(j1[0] + 1) * HALF] if k == 1 else T.p_z[:, 0:HALF],
                         T.part[:, j1[k] * HALF:(j1[k] + 1) * HALF], add).then_inc(S.o1 if last else S.ad, 1)
    sy.wait_ge(S.o1, 1)
    sy.dma_start(T.y[:, HALF:TK], T.ysb[:, HALF:TK]).then_inc(S.dn1, 16)
    sy.wait_ge(S.dn1, 16)
